import numpy as np, ml_dtypes
CORES = [78,86,94,102,110,118]
N = 6
BF = ml_dtypes.bfloat16
W, U, SH, B, T, DEL, LIM = 3072, 1536, 1, 192, 7, 3, 18
def parts(rng):
    return (rng.integers(0, 64, (N, 8, 16, W)), rng.integers(0, W, (N, 8, 16, U)), rng.integers(0, W, (N, 8, 16, B)), rng.integers(0, W, (N, 8, B)), rng.integers(0, 64, (N, 8, 16, B)))
def pack(x, canal, trail, cut, z):
    return {"x": x.reshape(N, 128, W).astype(np.float32).astype(BF), "canal": np.ascontiguousarray(canal.reshape(N, 128, U)).astype(np.int32), "trail": np.ascontiguousarray(trail.reshape(N, 128, B)).astype(np.int32),
            "cut": np.ascontiguousarray(cut).astype(np.int32), "z": z.reshape(N, 128, B).astype(np.float32).astype(BF)}
def setup_inputs(rng):
    return pack(*parts(rng))
def setup_inputs_spread(rng):
    def low(*shape): return np.minimum((W * rng.random(shape) ** 3).astype(np.int64), W - 1)
    def size(n): return np.minimum((64.0 ** rng.random((N, 8, 1, n)) * rng.random((N, 8, 16, n))).astype(np.int64), 63)
    return pack(size(W), low(N, 8, 16, U), low(N, 8, 16, B), low(N, 8, B), size(B))
def tips(rng, *shape):
    q = rng.random(shape)
    return np.where(q < 0.36, 0, np.where(q < 0.72, W - 1, rng.integers(0, W, shape)))
def setup_inputs_ends(rng):
    k = rng.random((N, 8, 1, W)); x = np.where(k < 0.2, 0, np.where(k < 0.4, 63, 63 * rng.integers(0, 2, (N, 8, 16, W))))
    one = (np.arange(16).reshape(1, 1, 16, 1) == rng.integers(0, 16, (N, 8, 1, W))) & (rng.random((N, 8, 1, W)) < 0.15)
    x = np.where(one, np.where(x == 63, 62, 1), x)
    for q in (1, N - 1): x[q] = np.where(rng.random((8, 1, W)) < 0.3, 32 + LIM + rng.integers(0, 3, (8, 1, W)), x[q])
    k = rng.random((N, 8, 1, B)); z = np.where(k < 0.3, 0, np.where(k < 0.45, 63, 63 * rng.integers(0, 2, (N, 8, 16, B))))
    for q in (0, 1, N - 1): z[q] = np.repeat(63 * rng.integers(0, 2, (8, 1, B)), 16, axis=1)
    z[:, :, :, B - 1] = 0
    canal, trail, cut = tips(rng, N, 8, 16, U), tips(rng, N, 8, 16, B), tips(rng, N, 8, B); cut[:, :, B - 1] = W - 1
    for r in range(N):
        for g in range(8):
            a = 2 * int(rng.integers(W // 8, W // 4)); b = a - 1; rows = rng.permutation(15)[:2]
            x[r, g, :, 0] = 0 if r in (0, 1, N - 1) else 63 * ((r + g) % 2)
            x[r, g, :, W - 1] = 63; x[r, g, :, a] = 63; x[r, g, :, b] = 63; x[r, g, int(rng.integers(0, 16)), b] = 62
            canal[r, g, :, U - 1] = W - 1; canal[r, g, rows[0], U - 1] = a; canal[r, g, rows[1], U - 1] = b
    w = 16 - DEL
    for q in (1, N - 1): trail[q, :, w] = np.where(z[q, :, 0] == 0, W - 1, 0)
    trail[1, 0, w, 0] = W - 1 - trail[1, 0, w, 0]
    trail[0, :, w] = np.where(z[0, :, 0] == 0, 0, W - 1)
    for q in range(2, N - 1):
        trail[q, 7, w] = np.where((trail[q, 7, w] >> SH) == U - 1, 0, trail[q, 7, w]); trail[q, 7, w, B - 1] = W - 1
    return pack(x, canal, trail, cut, z)
def setup_inputs_corners(rng):
    x, canal, trail, cut, z = parts(rng); s = int(rng.integers(0, 8)); H = 1 << SH
    for r in range(N):
        for g in range(8):
            kind = (r + g + s) % 8
            if kind == 0: cut[r, g] = (0, W - 1, int(rng.integers(0, W)))[r % 3]
            if kind == 1:
                u = rng.integers(0, U, (16, 1)); u[16 - DEL] = U - 1; u[17 - DEL if DEL > 1 else 0] = 0
                trail[r, g] = (u << SH) + rng.integers(0, H, (16, B))
            if kind == 2: trail[r, g] = (np.argsort(rng.random((16, U)), axis=1)[:, :B] << SH) + rng.integers(0, H, (16, B))
            if kind == 3:
                canal[r, g] = (np.arange(U)[None, :] << SH) + rng.integers(0, H, (16, U))
                cut[r, g] = rng.permutation(W)[:B]; trail[r, g] = cut[r, g][None, :]
            if kind == 4: x[r, g] = 30 + rng.integers(0, 4, (16, W)); z[r, g] = 30 + rng.integers(0, 4, (16, B))
            if kind == 5: x[r, g] = rng.integers(0, 4, (16, W)); z[r, g] = rng.integers(60, 64, (16, B))
            if kind == 6:
                at = np.argsort(rng.random((16, W)), axis=0); n = rng.integers(8, 10, (1, W)); sg = 2 * rng.integers(0, 2, (16, W)) - 1
                x[r, g] = 24 + sg * np.where(at < n, LIM + 1, LIM); z[r, g] = 24
            if kind == 7:
                x[r, g] = rng.integers(60, 64, (16, 4))[:, rng.integers(0, 4, W)]
                canal[r, g] = -np.sort(-canal[r, g], axis=0); canal[r, g, :, ::5] = canal[r, g, :1, ::5]
    return pack(x, canal, trail, cut, z)
def setup_inputs_full(rng):
    x, canal, trail, cut, z = parts(rng); w = 16 - DEL; w1 = (17 - DEL) % 16; H = 1 << SH; q = B // 4
    for r in range(N):
        for g in range(8):
            v = rng.integers(0, 64, W); y = np.full(B, 16); l = canal[r, g]; h = trail[r, g]
            if r == 0:
                h[w] = (rng.permutation(U)[:B] << SH) + rng.integers(0, H, B); v[h[w]] = rng.integers(40, 59, B)
            elif r == 1:
                o = rng.permutation(W - H); best = o[:B]; low = o[B:]
                v = rng.integers(0, 21, W); v[best] = rng.integers(25, 33, B)
                u = rng.permutation(U)[:B]; cut[r, g] = (u << SH) + rng.integers(0, H, B)
                l[:] = low[rng.integers(0, len(low), (16, U))]; l[rng.integers(0, 16, B), u] = best
                h[:] = rng.integers(0, W - H, (16, B))
                h[w, :B - 1] = (rng.permutation(U - 1)[:B - 1] << SH) + rng.integers(0, H, B - 1); h[w, B - 1] = W - 1
            elif r == 2:
                a = np.flatnonzero((v >= 16) & (v <= 32)); h[w] = a[rng.integers(0, len(a), B)]; h[w1] = a[rng.integers(0, len(a), B)]
                if g in (0, 3, 7):
                    far = np.flatnonzero(v >= 40); i = 0 if g == 0 else B - 1 if g == 7 else int(rng.integers(0, B))
                    h[w, i] = far[int(rng.integers(0, len(far)))]
            else:
                v = rng.integers(0, 63, W); v[0] = 63; v[W - 1] = 63
                y = rng.integers(0, 64, B); i = rng.permutation(B); u = rng.permutation(U - 1)[:2 * q]
                y[i[:q]] = 63; y[i[q:2 * q]] = 0; cut[r, g, i[:2 * q]] = (u << SH) + rng.integers(0, H, 2 * q)
                l[:, u[:q]] = W - 1; l[:, u[q:]] = rng.integers(1, W - 1, (16, q))
                l[rng.integers(0, 2, q), u[q:]] = 0; l[rng.integers(13, 16, q), u[q:]] = W - 1
            x[r, g] = v; z[r, g] = y
            if r > 2: x[r, g, int(rng.integers(0, 16)), 0] = 62
    return pack(x, canal, trail, cut, z)
def setup_inputs_meet(rng):
    x, canal, trail, cut, z = parts(rng)
    for r in range(N):
        for g in range(8):
            s = rng.permutation(W)[:64]; s[0] = W - 1
            canal[r, g] = s[rng.integers(0, 64, (16, U))]; trail[r, g] = s[rng.integers(0, 64, (16, B))]; cut[r, g] = s[rng.integers(0, 64, B)]
    return pack(x, canal, trail, cut, z)
def check_inputs(d):
    bad = []
    for k, hi in (("x", 63), ("canal", W - 1), ("trail", W - 1), ("cut", W - 1), ("z", 63)):
        a = np.asarray(d[k]).astype(np.float64)
        if not (np.min(a) >= 0 and np.max(a) <= hi): bad.append("range of " + k)
        if not np.all(a == np.floor(a)): bad.append("whole numbers in " + k)
    return bad
def reference(x, canal, trail, cut, z):
    X = x.astype(np.float32).astype(np.int64).reshape(N, 8, 16, W); C = canal.astype(np.int64).reshape(N, 8, 16, U); G = trail.astype(np.int64).reshape(N, 8, 16, B)
    V = cut.astype(np.int64).reshape(N, 8, B); Z = z.astype(np.float32).astype(np.int64).reshape(N, 8, 16, B); skips = np.zeros(N, np.int64)
    for t in range(T):
        lim = LIM + (skips & 3); skips = np.zeros(N, np.int64); come = np.zeros_like(Z); row = (t + 16 - DEL) % 16
        for r in range(N):
            for g in range(8):
                a, l, h, q = X[r, g], C[r, g], G[r, g], Z[r, g]
                k = l[:, V[r, g] >> SH]
                score = np.add.reduce(np.maximum(a[:, k] - q[:, None, :], 0), axis=0)
                c = np.min(np.where(score == np.max(score, axis=0), k, W), axis=0)
                cut_off = np.sum(np.abs(a[:, h] - q[:, None, :]) > lim[r], axis=0) >= 9
                w = h[row] + 0; skip = cut_off[row]; xw = a[:, w]; xc = a[:, c]
                first = np.zeros(B, bool); first[np.unique(w >> SH, return_index=True)[1]] = True
                new = np.where(skip, np.minimum(xw + 4, 63), (xw + q) >> 1)
                a[:, w[first]] = new[:, first]
                m = first & ~skip; u = w[m] >> SH
                l[:, u] = np.where(cut_off[:, m], l[:, u], h[:, m])
                h[:] = np.where(cut_off, k, h); h[t] = c
                a[:, c] = xc >> 1
                V[r, g] = c; skips[r] += np.sum(skip)
                come[(r + 1 + t % (N - 1)) % N, g] = (q + xc) >> 1
        Z = come
    return {"yx": X.reshape(N, 128, W).astype(np.float32).astype(BF), "yl": C.reshape(N, 128, U).astype(np.float32), "yg": G.reshape(N, 128, B).astype(np.float32)}

@@ -1,0 +1,461 @@
+from concourse.mybir import dt, AluOpType, AxisListType, ActivationFunctionType
+
+W, U, B, T_STEPS = 3072, 1536, 192, 7
+NB = B // 16
+STARTS = [sum(B - 16 * m for m in range(i)) for i in range(NB + 1)]
+RUN = STARTS[NB]
+CMID = 1536
+XB = 192
+ROWS = [(t + 13) % 16 for t in range(T_STEPS)]
+
+f32, b16, f16, i32, u16 = "float32", "bfloat16", "float16", "int32", "uint16"
+_S = {
+    "X": ([128, W + B], b16), "CN": ([128, 3840], f32), "TR": ([128, B], f16), "TRu": ([128, B], u16),
+    "xraw": ([128, W], b16), "craw": ([128, U], i32), "traw": ([128, B], i32), "zraw": ([128, B], b16), "vraw": ([128, B], i32),
+    "Ku": ([128, B], u16), "Kf": ([128, B], f32), "Kp": ([128, 6, 32], f16), "V": ([128, 6, 32], f16),
+    "Xg1": ([128, W], b16), "Xg2": ([128, W], b16), "M1": ([128, NB, 256], b16),
+    "A2": ([128, 3, 1024], b16), "IND": ([128, 3, 1024], b16), "AR": ([128, B], b16), "IR": ([128, B], b16),
+    "Sc": ([128, B], f32), "ci": ([128, NB], i32), "cm": ([128, NB], i32), "ch": ([128, NB], i32), "cf": ([128, NB], f32),
+    "CL": ([128, NB], u16), "VH": ([128, NB], u16), "UL": ([128, NB], u16), "ULf": ([128, 16], f32), "Dg": ([128, B], f16),
+    "ACh": ([128, B], f16), "E": ([128, RUN], b16), "EC": ([128, RUN], b16), "sg": ([128, B], f32), "xcut": ([128, B], b16),
+    "WD": ([128, B], f32), "WS": ([128, B], f32), "wu": ([128, 24], i32), "LU": ([128, NB], u16), "wb": ([128, NB], f32),
+    "SQ": ([128, RUN], b16), "SW": ([128, RUN], b16), "NF": ([128, 32], f32), "e1": ([128, 24], f32), "WU": ([128, 24], f32),
+    "LH": ([128, NB], u16), "LCf": ([128, NB], f32), "LC": ([128, NB], u16), "skb": ([128, NB], b16), "skr": ([128, B], b16),
+    "H": ([128, B], b16), "Q": ([128, B], b16), "mQ": ([128, B], b16),
+    "sm": ([128, B], f32), "tD": ([128, B], f32), "TRf": ([128, B], f32),
+    "Co": ([128, B], f32), "CG": ([128, B], f32), "cD": ([128, B], f32), "TF": ([128, B], f32),
+    "jnk": ([128, NB], f32), "Sa": ([128, 1], f32), "Si": ([128, 1], i32), "Sj": ([128, 1], i32),
+    "LIM": ([128, 1], f32), "LB": ([128, 1], f32), "CB": ([128, 1], f32),
+    "qi": ([128, 1], i32), "qa": ([128, 1], i32), "qm": ([128, 1], f32),
+    "half": ([128, 2], f32), "io1": ([128, 48], f32), "io2": ([128, 48], f32), "io3": ([128, 48], f32),
+    "REV": ([128, NB], u16), "RP": ([128, NB], u16), "ENDS": ([128, 2], u16), "DUM": ([128, 32], f32),
+    "J16": ([128, B], f32), "DM": ([128, B], f32), "RST": ([128, B], f32), "A0": ([128, B], f32), "MK": ([128, RUN], b16), "MB": ([128, RUN], b16),
+    "on": ([128, 144], f32), "on2": ([128, 144], f32), "BOf": ([128, 128], f32), "IDf": ([128, 128], f32), "sh0": ([128, 128], f32), "sh1": ([128, 128], f32),
+    "BOh": ([128, 128], f16), "BOb": ([128, 128], b16), "PD1": ([128, 144], b16), "PDN": ([128, 144], b16), "PDH": ([128, 144], f16),
+    "IDb": ([128, 128], b16), "NIb": ([128, 128], b16), "IDh": ([128, 128], f16), "IDm": ([128, T_STEPS * 128], f16), "RSL": ([128, T_STEPS * 128], f16),
+    "SWP": ([128, 512], f16), "zero": ([128, B], b16), "ONS": ([128, 128], b16), "vsh": ([128, B], i32), "vfh": ([128, B], f16), "vrf": ([128, B], f32),
+}
+for _t in range(T_STEPS):
+    _S["Z%d" % _t] = ([128, B], b16)
+    if _t < T_STEPS - 1:
+        _S["ZN%d" % _t] = ([128, B], b16)
+SCRATCH = {k: ("sbuf", s, d) for k, (s, d) in _S.items()}
+SCRATCH.update({
+    "PA": ("psum", [128, 1024], f32), "PB": ("psum", [128, 1024], f32),
+    "PZ": ("psum", [128, 512], f32), "PK": ("psum", [128, 512], f32), "PW": ("psum", [128, 512], f32), "PC": ("psum", [128, 512], f32),
+})
+SEMAPHORES = ["sv", "sp", "sa", "sg", "zsent"] + ["zs%d" % t for t in range(1, T_STEPS)] + ["d%d" % i for i in range(40)]
+
+
+def rank_program(g, core, T, topo):
+    rank = T.rank_of(core)
+    if rank is None:
+        return
+    O, AF = AluOpType, ActivationFunctionType
+    N = len(T.cores)
+    ENG = {"v": g.vector, "p": g.tensor, "a": g.scalar, "g": g, "s": g.sync}
+    cnt, known, wr, rd = {}, {}, {}, {}
+
+    def need(q, src, n):
+        if known.get((q, src), 0) < n:
+            known[(q, src)] = n
+            ENG[q].wait_ge(T.sem[src], n)
+
+    def deps(q, R, Wr, par):
+        own = "s" + q
+        for k in R:
+            if k in wr and not (q == "p" and wr[k][0] == own):
+                need(q, wr[k][0], wr[k][1])
+            if k[0] == "P":
+                for s, n in rd.get(k, {}).items():
+                    if s != own:
+                        need(q, s, n)
+        for k in Wr:
+            if k in wr and not (wr[k][0] == own and (par or q == "p")):
+                need(q, wr[k][0], wr[k][1])
+            for s, n in rd.get(k, {}).items():
+                if not (s == own and (par or q == "p")):
+                    need(q, s, n)
+
+    def note(src, n, R, Wr):
+        for k in R:
+            rd.setdefault(k, {})[src] = n
+        for k in Wr:
+            wr[k] = (src, n)
+            rd[k] = {}
+
+    def op(q, name, R, Wr, *a, par=False, **kw):
+        R, Wr = R.split(), Wr.split()
+        deps(q, R, Wr, par)
+        if q == "v":
+            e = g.vector
+            fn = {"tc": e.tensor_copy, "ts": e.tensor_scalar, "tt": e.tensor_tensor, "scan": e.tensor_tensor_scan,
+                  "ms": e.memset, "tr": e.transpose}[name]
+        elif q == "a":
+            fn = g.scalar.activation
+        elif q == "p":
+            fn = g.tensor.matmul
+        else:
+            fn = {"iota": g.iota, "sel": g.affine_select}[name]
+        src = "s" + q
+        cnt[src] = cnt.get(src, 0) + 1
+        fn(*a, **kw).then_inc(T.sem[src], 1)
+        note(src, cnt[src], R, Wr)
+
+    nd = [0]
+
+    def dma(q, R, Wr, out, in_):
+        R, Wr = R.split(), Wr.split()
+        deps(q, R, Wr, True)
+        s = "d%d" % nd[0]
+        nd[0] += 1
+        ENG[q].dma_start(out, in_).then_inc(T.sem[s], 16)
+        note(s, 16, R, Wr)
+        return s
+
+    def vtc(R, Wr, o, i, **k):
+        op("v", "tc", R, Wr, o, i, **k)
+
+    def vts(R, Wr, o, i, s1, o0, s2=None, o1=None, **k):
+        if o1 is None:
+            op("v", "ts", R, Wr, o, i, s1, None, o0, **k)
+        else:
+            op("v", "ts", R, Wr, o, i, s1, s2, o0, o1, **k)
+
+    def vtt(R, Wr, o, a, b, f, **k):
+        op("v", "tt", R, Wr, o, a, b, f, **k)
+
+    def act(R, Wr, o, i, f=AF.Copy, **k):
+        op("a", "act", R, Wr, o, i, f, **k)
+
+    def mm(R, Wr, o, l, r, st, sp):
+        op("p", "mm", R, Wr, o, l, r, st, sp)
+
+    dma("s", "", "craw0", T.craw[:, 0:768], T.canal[:, 0:768])
+    dma("a", "", "craw1", T.craw[:, 768:1536], T.canal[:, 768:1536])
+    op("v", "ms", "", "vraw", T.vraw[:], 0)
+    for j in range(8):
+        dma("sa"[j % 2], "vraw" if j < 2 else "", "vr%d" % j, T.vraw[16 * j:16 * j + 1, :], T.cut[j:j + 1, :])
+    VR = " ".join("vr%d" % j for j in range(8))
+    dma("s", "", "traw", T.traw[:], T.trail[:])
+    dma("a", "", "zraw", T.zraw[:], T.z[:])
+    for j in range(4):
+        dma("sa"[j % 2], "", "xraw%d" % j, T.xraw[:, 768 * j:768 * j + 768], T.x[:, 768 * j:768 * j + 768])
+    op("g", "iota", "", "qi", T.qi[:], [[1, 1]], 0, 1)
+    op("g", "iota", "", "J16", T.J16[:], [[0, 12], [1, 16]], 0, 0, allow_small_or_imprecise_dtypes=True)
+    op("g", "iota", "", "io1", T.io1[:], [[16, 48]], 0, 0, allow_small_or_imprecise_dtypes=True)
+    op("v", "ms", "", "on", T.on[:], 1.0)
+    op("v", "ms", "", "on2", T.on2[:], 0.0)
+    op("v", "ms", "on2", "on2", T.on2[:, 15::16], 1.0)
+    op("v", "ms", "", "fon", T.sh0[:], 1.0)
+    op("g", "sel", "on", "on", T.on[:, 0:128], T.on[:, 0:128], [[-16, 8], [0, 16]], O.is_ge, 0.0, 0, 1)
+    op("g", "sel", "on", "BOf", T.BOf[:], T.on[:, 0:128], [[16, 8], [0, 16]], O.is_ge, 0.0, 15, -1)
+    op("g", "sel", "on2", "on2", T.on2[:], T.on2[:], [[-16, 9], [0, 16]], O.is_ge, 0.0, 0, 1)
+    op("g", "sel", "on2", "on2", T.on2[:], T.on2[:], [[16, 9], [0, 16]], O.is_ge, 0.0, 15, -1)
+    op("g", "sel", "fon", "sh1", T.sh1[:], T.sh0[:], [[-1, 128]], O.is_equal, 0.0, -16, 1)
+    op("g", "sel", "fon sh1", "sh0", T.sh0[:], T.sh0[:], [[-1, 128]], O.is_equal, 0.0, 16, 1)
+    vts("qi", "qa", T.qa[:], T.qi[:], 15, O.bitwise_and)
+    vtc("qa", "qm", T.qm[:], T.qa[:])
+    vts("J16 qm", "DM", T.DM[:], T.J16[:], T.qm[:], O.is_equal)
+    vts("io1 qm", "io2", T.io2[:, 0:12], T.io1[:, 0:12], T.qm[:], O.add)
+    vts("io2", "REV", T.REV[:], T.io2[:, 0:12], -1.0, O.mult, 191.0, O.add)
+    vts("J16", "A0", T.A0[:], T.J16[:], 0.0, O.not_equal)
+    vtc("BOf", "BOh", T.BOh[:], T.BOf[:])
+    vts("io1", "RP", T.RP[:], T.io1[:, 0:12], 0.0625, O.mult)
+    vts("J16 qm", "IDf0", T.IDf[:], T.J16[:, 0:128], T.qm[:], O.is_equal)
+    vtt("IDf0 BOf", "IDf", T.IDf[:], T.IDf[:], T.BOf[:], O.mult)
+    act("IDf", "IDb", T.IDb[:], T.IDf[:])
+    act("IDf", "NIb", T.NIb[:], T.IDf[:], AF.Copy, scale=-1.0)
+    act("on2", "PDN", T.PDN[:], T.on2[:], AF.Copy, scale=-4096.0)
+    act("BOf", "BOb", T.BOb[:], T.BOf[:])
+    act("zraw REV", "Z0", T.Z0[:], T.zraw[:].indirect(T.REV[:]), AF.Copy, bias=float(XB))
+    vtc("IDf", "IDh", T.IDh[:], T.IDf[:])
+    for m in range(T_STEPS):
+        op("g", "sel", "BOh", "RSL%d" % m, T.RSL[:, 128 * m:128 * m + 128], T.BOh[:], [[-16, 8], [0, 16]], O.is_equal, 0.0, -ROWS[m], 1)
+        op("g", "sel", "IDh", "IDm%d" % m, T.IDm[:, 128 * m:128 * m + 128], T.IDh[:], [[0, 8], [1, 16]], O.not_equal, 0.0, -m, 0)
+    vts("vraw " + VR, "vsh", T.vsh[:], T.vraw[:], 1, O.arith_shift_right)
+    vtc("vsh", "vfh", T.vfh[:], T.vsh[:])
+    mm("BOh vfh", "PW", T.PW[:, 0:192], T.BOh[:], T.vfh[:], True, True)
+    act("PW", "vrf", T.vrf[:], T.PW[:, 0:192])
+    vtc("craw0", "CN", T.CN[:, 0:768], T.craw[:, 0:768])
+    vtt("vrf REV DM", "WD", T.WD[:], T.vrf[:].indirect(T.REV[:]), T.DM[:], O.mult)
+    op("v", "scan", "A0 WD", "WS", T.WS[:], T.A0[:], T.WD[:], 0.0, O.mult, O.add)
+    vtc("WS", "VH", T.VH[:], T.WS[:, 15::16])
+    vtc("craw1", "CN", T.CN[:, 768:1536], T.craw[:, 768:1536], par=True)
+    for j in range(3):
+        act("xraw%d" % j, "X", T.X[:, 768 * j:768 * j + 768], T.xraw[:, 768 * j:768 * j + 768], AF.Copy, bias=float(XB), par=True)
+    vts("xraw3", "X2", T.X[:, 2304:3072], T.xraw[:, 2304:3072], float(XB), O.add)
+    act("on2", "PD1", T.PD1[:], T.on2[:])
+    SWPS = "SWP00 SWP01 SWP10 SWP11"
+
+    def trail_list(j):
+        lo, hi = ((0, 128), (128, 192))[j]
+        vts("TR%d" % j, "TRu%d" % j, T.TRu[:, lo:hi], T.TR[:, lo:hi], float(CMID), O.add)
+
+    def consts_a():
+        vts("traw REV", "TR0 TR1", T.TR[:], T.traw[:].indirect(T.REV[:]), -float(CMID), O.add)
+        trail_list(0)
+        trail_list(1)
+        op("v", "ms", "", "zero", T.zero[:], 0.0)
+
+    def consts_b():
+        vts("qi", "Si", T.Si[:], T.qi[:], 16, O.bitwise_and)
+        vts("Si", "half", T.half[:, 1:2], T.Si[:], 0.0625, O.mult)
+        vts("half", "half0", T.half[:, 0:1], T.half[:, 1:2], -1.0, O.mult, 1.0, O.add)
+        vts("IDf half half0", "SWP00", T.SWP[:, 0:128], T.IDf[:], T.half[:, 0:1], O.mult, -1.0, O.mult)
+        vts("sh0 half half0", "SWP10", T.SWP[:, 256:384], T.sh0[:], T.half[:, 0:1], O.mult, -1.0, O.mult)
+        vts("sh1 half half0", "SWP01", T.SWP[:, 128:256], T.sh1[:], T.half[:, 1:2], O.mult, -1.0, O.mult)
+        vts("IDf half half0", "SWP11", T.SWP[:, 384:512], T.IDf[:], T.half[:, 1:2], O.mult, -1.0, O.mult)
+
+    def consts_c():
+        vts("J16", "RST0", T.RST[:], T.J16[:], 0.0, O.is_equal, 2.0e8, O.mult)
+        vts("RST0", "RST", T.RST[:], T.RST[:], -1.0e8, O.add)
+        op("v", "ms", "", "DUM", T.DUM[:], 0.0)
+        vts("io2", "DUM", T.DUM[:, 0:12], T.io2[:, 0:12], float(W), O.add)
+        vts("io2", "DUM", T.DUM[:, 12:24], T.io2[:, 0:12], float(U), O.add)
+        vtc("io2", "io3", T.io3[:, 0:2], T.io2[:, 0:2])
+        for lim in (12.0, 24.0):
+            vts("io2", "io1b", T.io1[:, 16:18], T.io2[:, 0:2], lim, O.is_ge, -12.0, O.mult)
+            vtt("io3 io1b", "io3", T.io3[:, 0:2], T.io3[:, 0:2], T.io1[:, 16:18], O.add)
+        vts("io3", "io1b", T.io1[:, 16:18], T.io3[:, 0:2], -8.0, O.mult, 192.0, O.add)
+        vts("io3", "io1c", T.io1[:, 32:34], T.io3[:, 0:2], 1.0, O.add)
+        vtt("io1b io1c", "io3", T.io3[:, 4:6], T.io1[:, 16:18], T.io1[:, 32:34], O.mult)
+        vts("io3", "ENDS", T.ENDS[:], T.io3[:, 4:6], -1.0, O.add)
+        vtc("on2", "PDH", T.PDH[:], T.on2[:])
+        op("v", "ms", "", "LIM", T.LIM[:], 18.5)
+        op("v", "ms", "", "CB", T.CB[:], -1700.0)
+
+    def consts_d():
+        op("v", "ms", "", "onb", T.ONS[:], 1.0 / 2048.0)
+        op("v", "ms", "", "MK", T.MK[:], 1.0)
+        for ii in range(NB):
+            vts("J16 qm MK", "MKs", T.MK[:, STARTS[ii]:STARTS[ii] + 16], T.J16[:, 0:16], T.qm[:], O.is_gt, par=True)
+        vts("MKs MK", "MB", T.MB[:], T.MK[:], -1.0e8, O.mult, 1.0e8, O.add)
+
+    XW = "X X2"
+    Xw = T.X[:, 0:W]
+    CNw = T.CN[:, 0:U]
+    CH = [(0, 64), (64, 128), (128, 192)]
+    XG2 = "Xg2.0 Xg2.1 Xg2.2"
+    D2 = [("PA", T.PA), ("PB", T.PB), ("PA", T.PA)]
+    CNT = [("PB", T.PB, 0), ("PB", T.PB, 64), ("PC", T.PC, 0)]
+
+    def replay_rows(t):
+        mm("RSL%d TR0 TR1" % t, "PW", T.PW[:, 0:192], T.RSL[:, 128 * t:128 * t + 128], T.TR[:], True, True)
+        mm("IDh TR0 TR1", "PC", T.PC[:, 192:384], T.IDh[:], T.TR[:], True, True)
+        act("PC", "TRf", T.TRf[:], T.PC[:, 192:384], AF.Copy, bias=float(CMID))
+
+    def trail_a(j):
+        lo, hi = ((0, 128), (128, 192))[j]
+        vtt("sm%d PW" % j, "tD%d" % j, T.tD[:, lo:hi], T.sm[:, lo:hi], T.PW[:, 256 + lo:256 + hi], O.mult)
+
+    def trail_b(j, out, nm):
+        lo, hi = ((0, 128), (128, 192))[j]
+        vtt("tD%d PK" % j, nm + "%d" % j, out[:, lo:hi], T.PK[:, 192 + lo:192 + hi], T.tD[:, lo:hi], O.subtract)
+
+    def g2(c):
+        act(XW + " TRu%d" % (c // 2), "Xg2.%d" % c, T.Xg2[:, 1024 * c:1024 * c + 1024], Xw.indirect(T.TRu[:, 64 * c:64 * c + 64]))
+
+    def diff(c, Zk, k0=0, k1=16):
+        nm, P = D2[c]
+        for k in range(k0, k1):
+            mm("IDb " + Zk, nm, P[:, 64 * k:64 * k + 64], T.IDb[:], T[Zk][:, 64 * c:64 * c + 64], True, False)
+            mm("NIb Xg2.%d" % c, nm, P[:, 64 * k:64 * k + 64], T.NIb[:], T.Xg2[:, 1024 * c + k:1024 * c + 1024:16], False, True)
+
+    def absd(c):
+        nm, P = D2[c]
+        act(nm, "A2.%d" % c, T.A2[:, c, :], P[:], AF.Abs)
+
+    def thr(c):
+        vts("A2.%d LIM" % c, "IND.%d" % c, T.IND[:, c, :], T.A2[:, c, :], T.LIM[:], O.is_gt)
+
+    def count(c):
+        nm, P, o = CNT[c]
+        for k in range(16):
+            mm("PD1 IND.%d" % c, nm, P[:, o:o + 64], T.PD1[:, 15 - k:143 - k], T.IND[:, c, 64 * k:64 * k + 64], k == 0, k == 15)
+
+    def ttmax(c, fill=()):
+        lo, hi = CH[c]
+        for k in range(16):
+            vtt("Xg1.%d PZ" % c, "M1.%d" % c, T.M1[:, 4 * c:4 * c + 4, k::16], T.Xg1[:, 1024 * c + k:1024 * c + 1024:16],
+                T.PZ[:, lo:hi], O.max, par=True)
+            if k % 4 == 3 and k // 4 < len(fill):
+                fill[k // 4]()
+
+    def score(c):
+        lo, hi = CH[c]
+        for p in range(16):
+            mm("PDN M1.%d" % c, "PK", T.PK[:, lo:hi], T.PDN[:, 15 - p:143 - p], T.M1[:, 4 * c:4 * c + 4, 16 * p:16 * p + 16],
+               False, c == 2 and p == 15)
+
+    outs = []
+
+    def fin(j):
+        c0 = 1536 * j
+        if j:
+            act(XW, "xo1", T.xraw[:, c0:c0 + 1536], T.X[:, c0:c0 + 1536], AF.Copy, bias=-float(XB))
+        else:
+            vts(XW, "xo0", T.xraw[:, c0:c0 + 1536], T.X[:, c0:c0 + 1536], -float(XB), O.add)
+        q = "sa"[j]
+        outs.append((q, dma(q, "xo%d" % j, "yx%d" % j, T.yx[:, c0:c0 + 1536], T.xraw[:, c0:c0 + 1536])))
+
+    for t in range(T_STEPS):
+        r = ROWS[t]
+        last = t == T_STEPS - 1
+        Zk, Zn = "Z%d" % t, "Z%d" % (t + 1)
+        Z = T[Zk]
+        vtc("CN VH", "Ku", T.Ku[:], CNw.indirect(T.VH[:]))
+        act("CN VH", "Kf", T.Kf[:], CNw.indirect(T.VH[:]), AF.Copy, bias=-float(CMID))
+        for c in (1, 2):
+            act(XW + " Ku", "Xg1.%d" % c, T.Xg1[:, 1024 * c:1024 * c + 1024], Xw.indirect(T.Ku[:, 64 * c:64 * c + 64]))
+        vtc(XW + " Ku", "Xg1.0", T.Xg1[:, 0:1024], Xw.indirect(T.Ku[:, 0:64]))
+        if not t:
+            consts_a()
+            mm("IDb " + Zk, "PZ", T.PZ[:, 0:192], T.IDb[:], Z[:], True, True)
+        else:
+            vtc("Sa", "Si", T.Si[:], T.Sa[:])
+            trail_a(1)
+            vts("Si", "Sj", T.Sj[:], T.Si[:], 3, O.bitwise_and)
+            trail_b(1, T.TR[:], "TR")
+            vts("Sj", "LIM", T.LIM[:], T.Sj[:], 18.5, O.add)
+            trail_list(1)
+        replay_rows(t)
+        mm("BOb zero", "PK", T.PK[:, 0:192], T.BOb[:], T.zero[:], True, False)
+        ttmax(0)
+        score(0)
+        if not t:
+            consts_b()
+            for c in range(2):
+                g2(c)
+                diff(c, Zk)
+        absd(0)
+        g2(2)
+        absd(1)
+        fills = [
+            lambda: [vts("Kf", "Kp", T.Kp[:, :, 16 * q:16 * q + 16], T.Kf[:, 96 * q:96 * q + 96], -1.0, O.mult, par=True) for q in range(2)],
+            lambda: op("v", "tr", "Kp", "V", T.V[:], T.Kp[:]),
+            lambda: vtt("PW DM", "WD", T.WD[:], T.PW[:, 0:192], T.DM[:], O.mult),
+            lambda: op("v", "scan", "A0 WD", "WS", T.WS[:], T.A0[:], T.WD[:], 0.0, O.mult, O.add),
+            lambda: vts("WS", "wi", T.wu[:, 0:12], T.WS[:, 15::16], float(CMID), O.add),
+            lambda: vts("wi", "ui", T.wu[:, 12:24], T.wu[:, 0:12], 1, O.arith_shift_right),
+            lambda: vtc("ui", "LU", T.LU[:], T.wu[:, 12:24]),
+            lambda: vts("ui", "wb", T.wb[:], T.wu[:, 12:24], -2.0, O.mult, float(CMID) - 0.5, O.add)]
+        ttmax(1, fills[:4])
+        for q in range(2):
+            for h in range(2):
+                mm("V " + SWPS, "PK", T.PK[:, 96 * q:96 * q + 96], T.SWP[:, 256 * h + 128 * q:256 * h + 128 * q + 128],
+                   T.V[:, :, 16 * h:16 * h + 16], False, False)
+        score(1)
+        ttmax(2, fills[4:])
+        score(2)
+        diff(2, Zk, 0, 8)
+        if not t:
+            consts_c()
+        thr(0)
+        count(0)
+        op("v", "scan", "RST PK", "Sc", T.Sc[:], T.RST[:], T.PK[:, 0:192], 0.0, O.max, O.min)
+        act("CN LU", "Co", T.Co[:], CNw.indirect(T.LU[:]), AF.Copy, bias=-float(CMID))
+        vts("Sc", "ci", T.ci[:], T.Sc[:, 15::16], float(CMID), O.add)
+        vts("ci", "cm", T.cm[:], T.ci[:], 4095, O.bitwise_and)
+        vts("cm", "cf", T.cf[:], T.cm[:], -float(CMID), O.add)
+        vtc("cm", "CL", T.CL[:], T.cm[:])
+        if not last:
+            vts("cm", "ch", T.ch[:], T.cm[:], 1, O.arith_shift_right)
+        vtt("cf RP DM", "Dg", T.Dg[:], T.cf[:].indirect(T.RP[:]), T.DM[:], O.mult)
+        if not last:
+            vtt(XW + " CL " + Zk, "sg", T.sg[:], Xw.indirect(T.CL[:]), Z[:], O.add)
+        mm("BOh Dg", "PZ", T.PZ[:, 192:384], T.BOh[:], T.Dg[:], True, True)
+        mm("IDm%d TR0 TR1" % t, "PK", T.PK[:, 192:384], T.IDm[:, 128 * t:128 * t + 128], T.TR[:], True, False)
+        mm("PDH Dg", "PK", T.PK[:, 192:384], T.PDH[:, 15 - t:143 - t], T.Dg[:], False, True)
+        if not last:
+            vtc("ch", "VH", T.VH[:], T.ch[:])
+            vts("sg", "ZN%d" % t, T["ZN%d" % t][:], T.sg[:], 0.5, O.mult, -0.25, O.add)
+            dst = T.cores[(rank + 1 + t % (N - 1)) % N]
+            rid, pid, _e = topo.addr(dst)
+            need("g", wr["ZN%d" % t][0], wr["ZN%d" % t][1])
+            g.remote_dma(T[Zn][:], T["ZN%d" % t][:], T.sem["zs%d" % (t + 1)], T.sem.zsent, pid, rid, topo.mask(core, dst))
+            src = T.cores[(rank - 1 - t % (N - 1)) % N]
+            note("zs%d" % (t + 1), len(topo.engines(src, core)), [], [Zn])
+        vtt("Co PC", "CG", T.CG[:], T.Co[:], T.PC[:, 192:384], O.subtract)
+        mm("IDb " + Zk, "PK", T.PK[:, 0:192], T.IDb[:], Z[:], True, False)
+        mm("NIb " + XG2, "PK", T.PK[:, 0:192], T.NIb[:], T.Xg2[:, r::16], False, True)
+        act("PK", "AR", T.AR[:], T.PK[:, 0:192], AF.Abs)
+        if not t:
+            consts_d()
+        vtc("PZ", "ACh", T.ACh[:], T.PZ[:, 192:384])
+        for ii in range(NB):
+            vts("ACh cf", "E", T.E[:, STARTS[ii]:STARTS[ii + 1]], T.ACh[:, 16 * ii:192], T.cf[:, ii:ii + 1], O.is_equal, par=True)
+        mm("IDb " + XG2, "PZ", T.PZ[:, 192:384], T.IDb[:], T.Xg2[:, r::16], True, False)
+        mm("IDb " + Zk, "PZ", T.PZ[:, 192:384], T.IDb[:], Z[:], False, True)
+        diff(2, Zk, 8, 16)
+        act("PZ", "H", T.H[:], T.PZ[:, 192:384], AF.Copy, scale=0.5, bias=-0.25)
+        for ii in range(NB):
+            act("PW wb", "SQ", T.SQ[:, STARTS[ii]:STARTS[ii + 1]], T.PW[:, 16 * ii:192], AF.Square, bias=T.wb[:, ii:ii + 1], par=True)
+        vts("AR LIM", "IR", T.IR[:], T.AR[:], T.LIM[:], O.is_gt)
+        vts(XG2, "Q", T.Q[:], T.Xg2[:, r::16], 4.0, O.add, XB + 63.0, O.min)
+        mm("BOb IR", "PC", T.PC[:, 192:384], T.BOb[:], T.IR[:], True, True)
+        for p in range(16):
+            mm("PD1 IR", "PC", T.PC[:, 384:396], T.PD1[:, 15 - p:143 - p], T.IR[:, p::16], p == 0, p == 15)
+        mm("IDb Q", "PZ", T.PZ[:, 0:192], T.IDb[:], T.Q[:], True, False)
+        mm("NIb H", "PZ", T.PZ[:, 0:192], T.NIb[:], T.H[:], False, True)
+        act(XW + " CL", "xcut", T.xcut[:], Xw.indirect(T.CL[:]), AF.Copy, scale=0.5, bias=XB / 2 - 0.25)
+        act("PC CB", "skr", T.skr[:], T.PC[:, 192:384], AF.Sigmoid, bias=T.CB[:], scale=200.0)
+        absd(2)
+        act("LIM", "LB", T.LB[:], T.LIM[:], AF.Copy, scale=-200.0)
+        act("A2.2 LB", "IND.2", T.IND[:, 2, :], T.A2[:, 2, :], AF.Sigmoid, bias=T.LB[:], scale=200.0)
+        op("v", "scan", "E MK MKs", "EC", T.EC[:], T.E[:], T.MK[:], 0.0, O.max, O.mult)
+        thr(1)
+        count(1)
+        for q in range(2):
+            mm("IDm%d Kp" % t, "PW", T.PW[:, 256 + 96 * q:352 + 96 * q], T.IDm[:, 128 * t:128 * t + 128], T.Kp[:, :, 16 * q:16 * q + 16], True, False)
+            mm("IDm%d TR0 TR1" % t, "PW", T.PW[:, 256 + 96 * q:352 + 96 * q], T.IDm[:, 128 * t:128 * t + 128], T.TR[:, 96 * q:96 * q + 96], False, True)
+        op("v", "scan", "SQ MB", "SW", T.SW[:], T.SQ[:], T.MB[:], 1.0e8, O.min, O.max)
+        vtt("EC ENDS DUM", "ULf", T.ULf[:], T.EC[:].indirect(T.ENDS[:, 0:1]), T.DUM[:, 0:16], O.mult)
+        vts("SW ENDS", "NF", T.NF[:], T.SW[:].indirect(T.ENDS[:]), 1.0, O.is_lt)
+        vtt("ULf cm", "ULg", T.ULf[:, 0:12], T.ULf[:, 0:12], T.cm[:], O.max)
+        vtt("NF DUM", "e1", T.e1[:], T.NF[:, 0:24], T.DUM[:, 0:24], O.mult)
+        vtc("ULg", "UL", T.UL[:], T.ULf[:, 0:12])
+        vtt("e1 wi ui", "WU", T.WU[:], T.e1[:], T.wu[:], O.max)
+        vts("PC", "skb", T.skb[:], T.PC[:, 384:396], 8.5, O.is_gt, 2048.0, O.mult)
+        vtc("WU", "LH", T.LH[:], T.WU[:, 0:12])
+        vtt("skr PZ", "mQ", T.mQ[:], T.skr[:], T.PZ[:, 0:192], O.mult)
+        vtt("skb WU", "LCf", T.LCf[:], T.skb[:], T.WU[:, 12:24], O.add)
+        vts("PB", "sm0", T.sm[:, 0:128], T.PB[:, 0:128], 8.5, O.is_gt)
+        vtt("mQ H LH", XW, T.X[:].indirect(T.LH[:]), T.mQ[:], T.H[:], O.add)
+        vtc("LCf", "LC", T.LC[:], T.LCf[:])
+        if not last:
+            trail_a(0)
+        vtc("xcut UL", XW, T.X[:].indirect(T.UL[:]), T.xcut[:])
+        if last:
+            for j in range(2):
+                fin(j)
+        if not last:
+            mm("onb skb", "PC", T.PC[:, 400:412], T.ONS[:], T.skb[:], True, True)
+            act("PC", "jnk Sa", T.jnk[:], T.PC[:, 400:412], AF.Copy, accum_out=T.Sa[:])
+        count(2)
+        if not last:
+            trail_b(0, T.TR[:], "TR")
+        vtt("sm0 CG", "cD0", T.cD[:, 0:128], T.sm[:, 0:128], T.CG[:, 0:128], O.mult)
+        if not last:
+            trail_list(0)
+            for c in range(2):
+                g2(c)
+            mm("IDb " + Zn, "PZ", T.PZ[:, 0:192], T.IDb[:], T[Zn][:], True, True)
+            diff(0, Zn)
+        vtt("cD0 TRf LC", "CN", T.CN[:].indirect(T.LC[:, 0:8]), T.cD[:, 0:128], T.TRf[:, 0:128], O.add)
+        vts("PC", "sm1", T.sm[:, 128:192], T.PC[:, 0:64], 8.5, O.is_gt)
+        vtt("sm1 CG", "cD1", T.cD[:, 128:192], T.sm[:, 128:192], T.CG[:, 128:192], O.mult)
+        vtt("cD1 TRf LC", "CN", T.CN[:].indirect(T.LC[:, 8:12]), T.cD[:, 128:192], T.TRf[:, 128:192], O.add)
+        if not last:
+            diff(1, Zn)
+    for j in range(2):
+        q = "sa"[j]
+        outs.append((q, dma(q, "CN", "yl%d" % j, T.yl[:, 768 * j:768 * j + 768], T.CN[:, 768 * j:768 * j + 768])))
+    for j in range(2):
+        trail_a(j)
+        trail_b(j, T.TF[:], "TF")
+    vts("TF0 TF1 REV", "go", T.sg[:], T.TF[:].indirect(T.REV[:]), float(CMID), O.add)
+    outs.append(("s", dma("s", "go", "yg", T.yg[:], T.sg[:])))
+    for q, s in outs:
+        need(q, s, 16)
+    g.wait_ge(T.sem.zsent, sum(len(topo.engines(core, T.cores[(rank + 1 + t % (N - 1)) % N])) for t in range(T_STEPS - 1)))

@@ -2,49 +2,60 @@ from concourse.mybir import dt, AluOpType, AxisListType, ActivationFunctionType
 
 W, U, B, T_STEPS = 3072, 1536, 192, 7
 NB = B // 16
-STARTS = [sum(B - 16 * m for m in range(i)) for i in range(NB + 1)]
-RUN = STARTS[NB]
 CMID = 1536
 XB = 192
 ROWS = [(t + 13) % 16 for t in range(T_STEPS)]
+BIG = 1.0e6
+RUN = 18
+ON_SCALAR = (0,)
+STEEP = 256.0
+GRID = 1.5 * 2.0 ** 35
 
 f32, b16, f16, i32, u16 = "float32", "bfloat16", "float16", "int32", "uint16"
 _S = {
-    "X": ([128, W + B], b16), "CN": ([128, 3840], f32), "TR": ([128, B], f16), "TRu": ([128, B], u16),
-    "xraw": ([128, W], b16), "craw": ([128, U], i32), "traw": ([128, B], i32), "zraw": ([128, B], b16), "vraw": ([128, B], i32),
-    "Ku": ([128, B], u16), "Kf": ([128, B], f32), "Kp": ([128, 6, 32], f16), "V": ([128, 6, 32], f16),
-    "Xg1": ([128, W], b16), "Xg2": ([128, W], b16), "M1": ([128, NB, 256], b16),
-    "A2": ([128, 3, 1024], b16), "IND": ([128, 3, 1024], b16), "AR": ([128, B], b16), "IR": ([128, B], b16),
-    "Sc": ([128, B], f32), "ci": ([128, NB], i32), "cm": ([128, NB], i32), "ch": ([128, NB], i32), "cf": ([128, NB], f32),
-    "CL": ([128, NB], u16), "VH": ([128, NB], u16), "UL": ([128, NB], u16), "ULf": ([128, 16], f32), "Dg": ([128, B], f16),
-    "ACh": ([128, B], f16), "E": ([128, RUN], b16), "EC": ([128, RUN], b16), "sg": ([128, B], f32), "xcut": ([128, B], b16),
-    "WD": ([128, B], f32), "WS": ([128, B], f32), "wu": ([128, 24], i32), "LU": ([128, NB], u16), "wb": ([128, NB], f32),
-    "SQ": ([128, RUN], b16), "SW": ([128, RUN], b16), "NF": ([128, 32], f32), "e1": ([128, 24], f32), "WU": ([128, 24], f32),
-    "LH": ([128, NB], u16), "LCf": ([128, NB], f32), "LC": ([128, NB], u16), "skb": ([128, NB], b16), "skr": ([128, B], b16),
-    "H": ([128, B], b16), "Q": ([128, B], b16), "mQ": ([128, B], b16),
-    "sm": ([128, B], f32), "tD": ([128, B], f32), "TRf": ([128, B], f32),
-    "Co": ([128, B], f32), "CG": ([128, B], f32), "cD": ([128, B], f32), "TF": ([128, B], f32),
-    "jnk": ([128, NB], f32), "Sa": ([128, 1], f32), "Si": ([128, 1], i32), "Sj": ([128, 1], i32),
-    "LIM": ([128, 1], f32), "LB": ([128, 1], f32), "CB": ([128, 1], f32),
-    "qi": ([128, 1], i32), "qa": ([128, 1], i32), "qm": ([128, 1], f32),
-    "half": ([128, 2], f32), "io1": ([128, 48], f32), "io2": ([128, 48], f32), "io3": ([128, 48], f32),
-    "REV": ([128, NB], u16), "RP": ([128, NB], u16), "ENDS": ([128, 2], u16), "DUM": ([128, 32], f32),
-    "J16": ([128, B], f32), "DM": ([128, B], f32), "RST": ([128, B], f32), "A0": ([128, B], f32), "MK": ([128, RUN], b16), "MB": ([128, RUN], b16),
-    "on": ([128, 144], f32), "on2": ([128, 144], f32), "BOf": ([128, 128], f32), "IDf": ([128, 128], f32), "sh0": ([128, 128], f32), "sh1": ([128, 128], f32),
-    "BOh": ([128, 128], f16), "BOb": ([128, 128], b16), "PD1": ([128, 144], b16), "PDN": ([128, 144], b16), "PDH": ([128, 144], f16),
-    "IDb": ([128, 128], b16), "NIb": ([128, 128], b16), "IDh": ([128, 128], f16), "IDm": ([128, T_STEPS * 128], f16), "RSL": ([128, T_STEPS * 128], f16),
-    "SWP": ([128, 512], f16), "zero": ([128, B], b16), "ONS": ([128, 128], b16), "vsh": ([128, B], i32), "vfh": ([128, B], f16), "vrf": ([128, B], f32),
+    "X": ([128, W + 2 * B], b16), "CN": ([128, 3840], f32), "TR": ([128, B], f16), "TRu": ([128, B], u16),
+    "craw": ([128, U], i32), "traw": ([128, B], i32), "vraw": ([128, B], i32), "vh": ([128, B], f16),
+    "Z": ([128, 2 * B], b16), "Kh": ([128, B], f16), "V": ([128, 32, 6], f16), "KT": ([128, B], u16),
+    "M": ([128, 8, 2 * B], b16), "key": ([128, B], f32), "Sc": ([128, B], f32), "RST": ([128, B], f32),
+    "Wt": ([128, B], f16), "St": ([128, B], b16),
+    "Xg": ([128, W], b16), "A2": ([128, 3, 960], b16), "IND": ([128, 3, 960], b16),
+    "AR": ([128, B], b16), "IR": ([128, B], b16), "sr": ([128, B], b16), "sev": ([128, B], b16), "Sa": ([128, 1], f32),
+    "ci": ([128, NB], f32), "cm": ([128, NB], f16), "cf": ([128, NB], f16),
+    "CL": ([128, NB], u16), "VH": ([128, NB], u16), "UL": ([128, NB], u16), "LU": ([128, NB], u16), "LH": ([128, NB], u16),
+    "LC": ([128, NB], u16), "LCf": ([128, NB], f32), "ul": ([128, NB], f32), "wf": ([128, NB], f16),
+    "crow": ([128, B], f16), "urow": ([128, B], f16), "Co": ([128, B], f16),
+    "Ew": ([128, NB, NB, RUN], b16), "Ec": ([128, NB, NB, RUN], b16), "Fw": ([128, NB * RUN], f32), "Fc": ([128, NB * RUN], f32),
+    "xw": ([128, B], b16), "LW": ([128, NB], u16), "xc": ([128, B], b16), "xcut": ([128, B], b16),
+    "t1": ([128, B], b16), "t2": ([128, B], b16), "Mid": ([128, B], f32), "cD": ([128, B], f32), "tD": ([128, B], f32), "TF": ([128, B], f32),
+    "Si": ([128, 1], i32), "Sj": ([128, 1], i32), "LIM": ([128, 8], f32), "NLIM": ([128, 8], f32),
+    "IOTA": ([128, W], f32), "qi": ([128, 1], i32), "qa": ([128, 1], i32), "qm": ([128, 1], f32), "half": ([128, 2], f32),
+    "J16": ([128, 16], f32), "lane": ([128, NB], f32), "RS": ([128, NB * RUN], f32), "NM": ([128, NB * RUN], b16),
+    "on": ([128, 144], f32), "on2": ([128, 144], f32), "BOf": ([128, 128], f32), "IDf": ([128, 128], f32),
+    "sh0": ([128, 128], f32), "sh1": ([128, 128], f32), "ONf": ([128, 128], f32), "SWP": ([128, 512], b16), "BO": ([128, 128], b16),
+    "PD1": ([128, 144], b16), "PDN": ([128, 144], b16), "PDS": ([128, 144], b16), "PDC": ([128, 144], b16),
+    "SW4": ([128, 512], b16), "HM": ([128, T_STEPS, 128], b16), "NHM": ([128, T_STEPS, 128], b16),
+    "cmid": ([128, B], b16), "cxb": ([128, B], b16), "c508": ([128, B], b16),
 }
-for _t in range(T_STEPS):
-    _S["Z%d" % _t] = ([128, B], b16)
-    if _t < T_STEPS - 1:
-        _S["ZN%d" % _t] = ([128, B], b16)
+IDS = {"ID": 1.0, "NID": -1.0, "NHI": -0.5, "I512": 512.0, "I4": 4096.0, "I8": 8192.0}
+for _k in IDS:
+    _S[_k] = ([128, 128], b16)
+for _t in range(1, T_STEPS):
+    _S["ZI%d" % _t] = ([128, B], b16)
+    _S["ZO%d" % _t] = ([128, B], b16)
 SCRATCH = {k: ("sbuf", s, d) for k, (s, d) in _S.items()}
 SCRATCH.update({
-    "PA": ("psum", [128, 1024], f32), "PB": ("psum", [128, 1024], f32),
-    "PZ": ("psum", [128, 512], f32), "PK": ("psum", [128, 512], f32), "PW": ("psum", [128, 512], f32), "PC": ("psum", [128, 512], f32),
+    "PA": ("psum", [128, 1024], f32), "PB": ("psum", [128, 1024], f32), "PK": ("psum", [128, 512], f32),
+    "PF": ("psum", [128, 512], f32), "PU": ("psum", [128, 512], f32), "PC": ("psum", [128, 512], f32),
 })
 SEMAPHORES = ["sv", "sp", "sa", "sg", "zsent"] + ["zs%d" % t for t in range(1, T_STEPS)] + ["d%d" % i for i in range(40)]
+
+FIRST = "wt g0 cn0 wl cn1 cn2 cn3 lw mid kr kt kl ko"
+STEP = """
+d0a xw mx0 mx1 mx2 dr d0b mx3 mx4 s0 g1 ar g2 s1 ir d1a mx5 mx6 lu ab0 d1b s2 mx7 s3 s4 br s5 sr s6 ulf d2a urow
+ew11 s7 ew10 ew9 ew8 ew7 tp ew6 sc ew5 wf th0 ci ew4 ew3 d2b p2 p1 cm ew2 t2 cw ab2 ew1 ew0 ab1 st vh cl
+fow sk crow n0 th2 fw cf lcf lh n2 co sa lc xc gs t1 th1 n1 ec11 ec10 ec9 ec8 ec7 ec6 si ec5 pd zn ec4 ec3 q1 sev xcut ec2 send ec1 sj ec0
+foc xr cd q2 td cs ol fc tr og ul tru xk ox nlim +kr +mid +kt +wt +za lim +kl +zb +wl +g0 +lw +ko
+"""
 
 
 def rank_program(g, core, T, topo):
@@ -61,12 +72,15 @@ def rank_program(g, core, T, topo):
             known[(q, src)] = n
             ENG[q].wait_ge(T.sem[src], n)
 
+    def keys(names):
+        return [k.split(":")[0] for k in names.split()]
+
     def deps(q, R, Wr, par):
         own = "s" + q
         for k in R:
             if k in wr and not (q == "p" and wr[k][0] == own):
                 need(q, wr[k][0], wr[k][1])
-            if k[0] == "P":
+            if k[0] == "@":
                 for s, n in rd.get(k, {}).items():
                     if s != own:
                         need(q, s, n)
@@ -85,7 +99,7 @@ def rank_program(g, core, T, topo):
             rd[k] = {}
 
     def op(q, name, R, Wr, *a, par=False, **kw):
-        R, Wr = R.split(), Wr.split()
+        R, Wr = keys(R), keys(Wr)
         deps(q, R, Wr, par)
         if q == "v":
             e = g.vector
@@ -105,7 +119,7 @@ def rank_program(g, core, T, topo):
     nd = [0]
 
     def dma(q, R, Wr, out, in_):
-        R, Wr = R.split(), Wr.split()
+        R, Wr = keys(R), keys(Wr)
         deps(q, R, Wr, True)
         s = "d%d" % nd[0]
         nd[0] += 1
@@ -125,337 +139,278 @@ def rank_program(g, core, T, topo):
     def vtt(R, Wr, o, a, b, f, **k):
         op("v", "tt", R, Wr, o, a, b, f, **k)
 
+    def vms(Wr, o, c, **k):
+        op("v", "ms", "", Wr, o, c, **k)
+
+    def scan(R, Wr, o, a, b, o0, o1):
+        op("v", "scan", R, Wr, o, a, b, 0.0, o0, o1)
+
     def act(R, Wr, o, i, f=AF.Copy, **k):
         op("a", "act", R, Wr, o, i, f, **k)
 
     def mm(R, Wr, o, l, r, st, sp):
         op("p", "mm", R, Wr, o, l, r, st, sp)
 
-    dma("s", "", "craw0", T.craw[:, 0:768], T.canal[:, 0:768])
-    dma("a", "", "craw1", T.craw[:, 768:1536], T.canal[:, 768:1536])
-    op("v", "ms", "", "vraw", T.vraw[:], 0)
-    for j in range(8):
-        dma("sa"[j % 2], "vraw" if j < 2 else "", "vr%d" % j, T.vraw[16 * j:16 * j + 1, :], T.cut[j:j + 1, :])
-    VR = " ".join("vr%d" % j for j in range(8))
-    dma("s", "", "traw", T.traw[:], T.trail[:])
-    dma("a", "", "zraw", T.zraw[:], T.z[:])
+    def mms(bank, o, terms):
+        for i, (R, l, r) in enumerate(terms):
+            mm(R, bank, o, l, r, i == 0, i == len(terms) - 1)
+
+    def sel(R, Wr, o, i, pat, cmp, base, mult):
+        op("g", "sel", R, Wr, o, i, pat, cmp, 0.0, base, mult)
+
+    def iota(Wr, o, pat, base, mult):
+        op("g", "iota", "", Wr, o, pat, base, mult, allow_small_or_imprecise_dtypes=True)
+
+    XW = "X0 X1 X2 X3"
+    CW = "CN0 CN1 CN2 CN3"
+    dma("s", "", "vraw", T.vraw[0:8, :], T.cut[:])
+    dma("a", "", "traw", T.traw[:], T.trail[:])
     for j in range(4):
-        dma("sa"[j % 2], "", "xraw%d" % j, T.xraw[:, 768 * j:768 * j + 768], T.x[:, 768 * j:768 * j + 768])
+        dma("sa"[j % 2], "", "X%d" % j, T.X[:, 768 * j:768 * j + 768], T.x[:, 768 * j:768 * j + 768])
+    dma("s", "", "Za", T.Z[:, 0:B], T.z[:])
+    dma("a", "", "Zb", T.Z[:, B:2 * B], T.z[:])
+    for j in range(4):
+        dma("sa"[j % 2], "", "craw%d" % j, T.craw[:, 384 * j:384 * j + 384], T.canal[:, 384 * j:384 * j + 384])
     op("g", "iota", "", "qi", T.qi[:], [[1, 1]], 0, 1)
-    op("g", "iota", "", "J16", T.J16[:], [[0, 12], [1, 16]], 0, 0, allow_small_or_imprecise_dtypes=True)
-    op("g", "iota", "", "io1", T.io1[:], [[16, 48]], 0, 0, allow_small_or_imprecise_dtypes=True)
-    op("v", "ms", "", "on", T.on[:], 1.0)
-    op("v", "ms", "", "on2", T.on2[:], 0.0)
-    op("v", "ms", "on2", "on2", T.on2[:, 15::16], 1.0)
-    op("v", "ms", "", "fon", T.sh0[:], 1.0)
-    op("g", "sel", "on", "on", T.on[:, 0:128], T.on[:, 0:128], [[-16, 8], [0, 16]], O.is_ge, 0.0, 0, 1)
-    op("g", "sel", "on", "BOf", T.BOf[:], T.on[:, 0:128], [[16, 8], [0, 16]], O.is_ge, 0.0, 15, -1)
-    op("g", "sel", "on2", "on2", T.on2[:], T.on2[:], [[-16, 9], [0, 16]], O.is_ge, 0.0, 0, 1)
-    op("g", "sel", "on2", "on2", T.on2[:], T.on2[:], [[16, 9], [0, 16]], O.is_ge, 0.0, 15, -1)
-    op("g", "sel", "fon", "sh1", T.sh1[:], T.sh0[:], [[-1, 128]], O.is_equal, 0.0, -16, 1)
-    op("g", "sel", "fon sh1", "sh0", T.sh0[:], T.sh0[:], [[-1, 128]], O.is_equal, 0.0, 16, 1)
+    iota("J16", T.J16[:], [[1, 16]], 0, 0)
+    iota("lane", T.lane[:], [[32, NB]], W - CMID, 0)
+    vms("on", T.on[:], 1.0)
+    vms("fon", T.sh0[:], 1.0)
+    vms("on2", T.on2[:], 0.0)
+    vms("cmid", T.cmid[:], float(CMID))
+    vms("RST", T.RST[:], -1.0e8)
+    vms("on2", T.on2[:, 15::16], 1.0)
+    vms("RST", T.RST[:, 0::16], 1.0e8)
+    sel("fon", "IDf", T.IDf[:], T.sh0[:], [[-1, 128]], O.is_equal, 0, 1)
+    sel("on", "PDC", T.PDC[0:8, :], T.on[0:8, :], [[1, 144]], O.is_equal, -15, -16)
+    sel("fon", "sh1", T.sh1[:], T.sh0[:], [[-1, 128]], O.is_equal, -16, 1)
+    sel("fon", "sh0", T.sh0[:], T.sh0[:], [[-1, 128]], O.is_equal, 16, 1)
+    iota("IO0", T.IOTA[:, 0:768], [[1, 768]], -CMID, 0)
+    sel("on2", "on2", T.on2[:], T.on2[:], [[-16, 9], [0, 16]], O.is_ge, 0, 1)
+    sel("on", "on", T.on[:, 0:128], T.on[:, 0:128], [[-16, 8], [0, 16]], O.is_ge, 0, 1)
+    sel("on2", "on2", T.on2[:], T.on2[:], [[16, 9], [0, 16]], O.is_ge, 15, -1)
+    sel("on", "BOf", T.BOf[:], T.on[:, 0:128], [[16, 8], [0, 16]], O.is_ge, 15, -1)
     vts("qi", "qa", T.qa[:], T.qi[:], 15, O.bitwise_and)
+    vts("qi", "Si", T.Si[:], T.qi[:], 16, O.bitwise_and)
+    vms("cxb", T.cxb[:], -float(XB))
     vtc("qa", "qm", T.qm[:], T.qa[:])
-    vts("J16 qm", "DM", T.DM[:], T.J16[:], T.qm[:], O.is_equal)
-    vts("io1 qm", "io2", T.io2[:, 0:12], T.io1[:, 0:12], T.qm[:], O.add)
-    vts("io2", "REV", T.REV[:], T.io2[:, 0:12], -1.0, O.mult, 191.0, O.add)
-    vts("J16", "A0", T.A0[:], T.J16[:], 0.0, O.not_equal)
-    vtc("BOf", "BOh", T.BOh[:], T.BOf[:])
-    vts("io1", "RP", T.RP[:], T.io1[:, 0:12], 0.0625, O.mult)
-    vts("J16 qm", "IDf0", T.IDf[:], T.J16[:, 0:128], T.qm[:], O.is_equal)
-    vtt("IDf0 BOf", "IDf", T.IDf[:], T.IDf[:], T.BOf[:], O.mult)
-    act("IDf", "IDb", T.IDb[:], T.IDf[:])
-    act("IDf", "NIb", T.NIb[:], T.IDf[:], AF.Copy, scale=-1.0)
-    act("on2", "PDN", T.PDN[:], T.on2[:], AF.Copy, scale=-4096.0)
-    act("BOf", "BOb", T.BOb[:], T.BOf[:])
-    act("zraw REV", "Z0", T.Z0[:], T.zraw[:].indirect(T.REV[:]), AF.Copy, bias=float(XB))
-    vtc("IDf", "IDh", T.IDh[:], T.IDf[:])
-    for m in range(T_STEPS):
-        op("g", "sel", "BOh", "RSL%d" % m, T.RSL[:, 128 * m:128 * m + 128], T.BOh[:], [[-16, 8], [0, 16]], O.is_equal, 0.0, -ROWS[m], 1)
-        op("g", "sel", "IDh", "IDm%d" % m, T.IDm[:, 128 * m:128 * m + 128], T.IDh[:], [[0, 8], [1, 16]], O.not_equal, 0.0, -m, 0)
-    vts("vraw " + VR, "vsh", T.vsh[:], T.vraw[:], 1, O.arith_shift_right)
-    vtc("vsh", "vfh", T.vfh[:], T.vsh[:])
-    mm("BOh vfh", "PW", T.PW[:, 0:192], T.BOh[:], T.vfh[:], True, True)
-    act("PW", "vrf", T.vrf[:], T.PW[:, 0:192])
-    vtc("craw0", "CN", T.CN[:, 0:768], T.craw[:, 0:768])
-    vtt("vrf REV DM", "WD", T.WD[:], T.vrf[:].indirect(T.REV[:]), T.DM[:], O.mult)
-    op("v", "scan", "A0 WD", "WS", T.WS[:], T.A0[:], T.WD[:], 0.0, O.mult, O.add)
-    vtc("WS", "VH", T.VH[:], T.WS[:, 15::16])
-    vtc("craw1", "CN", T.CN[:, 768:1536], T.craw[:, 768:1536], par=True)
-    for j in range(3):
-        act("xraw%d" % j, "X", T.X[:, 768 * j:768 * j + 768], T.xraw[:, 768 * j:768 * j + 768], AF.Copy, bias=float(XB), par=True)
-    vts("xraw3", "X2", T.X[:, 2304:3072], T.xraw[:, 2304:3072], float(XB), O.add)
-    act("on2", "PD1", T.PD1[:], T.on2[:])
-    SWPS = "SWP00 SWP01 SWP10 SWP11"
+    vts("Si", "half1", T.half[:, 1:2], T.Si[:], 0.0625, O.mult)
+    vms("c508", T.c508[:], -508.0)
+    vts("half1", "half0", T.half[:, 0:1], T.half[:, 1:2], -1.0, O.mult, 1.0, O.add)
+    vms("NMe", T.NM[:], 2048.0)
+    vms("RS", T.RS[:], BIG)
+    vms("ONf", T.ONf[:], 1.0 / 16.0)
+    vms("LIM0", T.LIM[:], 18.5)
+    vms("NLIM0", T.NLIM[:], -18.5 * STEEP)
+    vms("RS", T.RS[:, 0::RUN], -BIG)
+    vms("NMe", T.NM[:, RUN - 1::RUN], -30720.0)
+    for E in ("Ew", "Ec"):
+        for j in (0, RUN - 1):
+            vms(E + "z", T[E][:, :, :, j], 0.0, par=True)
+    vts("lane qm", "lane", T.lane[:], T.lane[:], T.qm[:], O.add, T.qm[:], O.add)
+    for b in range(NB):
+        vts("J16 qm NMe", "NM0", T.NM[:, RUN * b + 1:RUN * b + 17], T.J16[:], T.qm[:], O.is_ge, -4096.0, O.mult, par=True)
+    vtc("lane RS", "RS", T.RS[:, RUN - 1::RUN], T.lane[:])
+    vts("NM0 NMe", "NM", T.NM[:], T.NM[:], -2048.0, O.add)
+    for k, s in IDS.items():
+        act("IDf", k, T[k][:], T.IDf[:], AF.Copy, scale=s)
+    vts("vraw", "vh", T.vh[0:8, :], T.vraw[0:8, :], -float(CMID), O.add)
+    for p in range(16):
+        mm("PDC vh", "@U:s", T.PU[:, 256:256 + NB], T.PDC[0:8, 15 - p:143 - p], T.vh[0:8, p::16], p == 0, p == 15)
+    vtc("traw", "TRu", T.TRu[:], T.traw[:])
+    vts("traw", "TR", T.TR[:], T.traw[:], -float(CMID), O.add)
+    vts("@U:s", "VH", T.VH[:], T.PU[:, 256:256 + NB], CMID - 0.5, O.add, 0.5, O.mult)
+    act("IO0", "IO1", T.IOTA[:, 768:1536], T.IOTA[:, 0:768], AF.Copy, bias=768.0)
+    vts("IDf half0", "SWP", T.SWP[:, 0:128], T.IDf[:], T.half[:, 0:1], O.mult)
+    vts("IDf half1", "SWP", T.SWP[:, 384:512], T.IDf[:], T.half[:, 1:2], O.mult, par=True)
+    vts("sh1 half1", "SWP", T.SWP[:, 128:256], T.sh1[:], T.half[:, 1:2], O.mult, par=True)
+    vts("sh0 half0", "SWP", T.SWP[:, 256:384], T.sh0[:], T.half[:, 0:1], O.mult, par=True)
+    act("SWP", "SW4", T.SW4[:], T.SWP[:], AF.Copy, scale=4096.0)
+    vts("IO0", "IO2", T.IOTA[:, 1536:2304], T.IOTA[:, 0:768], 1536.0, O.add)
+    vts("IO0", "IO3", T.IOTA[:, 2304:W], T.IOTA[:, 0:768], 2304.0, O.add)
+    IO = "IO0 IO1 IO2 IO3"
+    for k, s in (("PDN", -4096.0), ("PD1", 1.0), ("PDS", 1.0 / 16.0)):
+        vts("on2", k, T[k][:], T.on2[:], s, O.mult)
+    act("BOf", "BO", T.BO[:], T.BOf[:], AF.Sigmoid, scale=STEEP, bias=-STEEP / 2)
+    for t in range(T_STEPS):
+        sel("ID", "HM%d" % t, T.HM[:, t, :], T.ID[:], [[0, 8], [1, 16]], O.not_equal, -t, 0)
+        sel("NID", "NHM%d" % t, T.NHM[:, t, :], T.NID[:], [[0, 8], [1, 16]], O.not_equal, -t, 0)
 
-    def trail_list(j):
-        lo, hi = ((0, 128), (128, 192))[j]
-        vts("TR%d" % j, "TRu%d" % j, T.TRu[:, lo:hi], T.TR[:, lo:hi], float(CMID), O.add)
-
-    def consts_a():
-        vts("traw REV", "TR0 TR1", T.TR[:], T.traw[:].indirect(T.REV[:]), -float(CMID), O.add)
-        trail_list(0)
-        trail_list(1)
-        op("v", "ms", "", "zero", T.zero[:], 0.0)
-
-    def consts_b():
-        vts("qi", "Si", T.Si[:], T.qi[:], 16, O.bitwise_and)
-        vts("Si", "half", T.half[:, 1:2], T.Si[:], 0.0625, O.mult)
-        vts("half", "half0", T.half[:, 0:1], T.half[:, 1:2], -1.0, O.mult, 1.0, O.add)
-        vts("IDf half half0", "SWP00", T.SWP[:, 0:128], T.IDf[:], T.half[:, 0:1], O.mult, -1.0, O.mult)
-        vts("sh0 half half0", "SWP10", T.SWP[:, 256:384], T.sh0[:], T.half[:, 0:1], O.mult, -1.0, O.mult)
-        vts("sh1 half half0", "SWP01", T.SWP[:, 128:256], T.sh1[:], T.half[:, 1:2], O.mult, -1.0, O.mult)
-        vts("IDf half half0", "SWP11", T.SWP[:, 384:512], T.IDf[:], T.half[:, 1:2], O.mult, -1.0, O.mult)
-
-    def consts_c():
-        vts("J16", "RST0", T.RST[:], T.J16[:], 0.0, O.is_equal, 2.0e8, O.mult)
-        vts("RST0", "RST", T.RST[:], T.RST[:], -1.0e8, O.add)
-        op("v", "ms", "", "DUM", T.DUM[:], 0.0)
-        vts("io2", "DUM", T.DUM[:, 0:12], T.io2[:, 0:12], float(W), O.add)
-        vts("io2", "DUM", T.DUM[:, 12:24], T.io2[:, 0:12], float(U), O.add)
-        vtc("io2", "io3", T.io3[:, 0:2], T.io2[:, 0:2])
-        for lim in (12.0, 24.0):
-            vts("io2", "io1b", T.io1[:, 16:18], T.io2[:, 0:2], lim, O.is_ge, -12.0, O.mult)
-            vtt("io3 io1b", "io3", T.io3[:, 0:2], T.io3[:, 0:2], T.io1[:, 16:18], O.add)
-        vts("io3", "io1b", T.io1[:, 16:18], T.io3[:, 0:2], -8.0, O.mult, 192.0, O.add)
-        vts("io3", "io1c", T.io1[:, 32:34], T.io3[:, 0:2], 1.0, O.add)
-        vtt("io1b io1c", "io3", T.io3[:, 4:6], T.io1[:, 16:18], T.io1[:, 32:34], O.mult)
-        vts("io3", "ENDS", T.ENDS[:], T.io3[:, 4:6], -1.0, O.add)
-        vtc("on2", "PDH", T.PDH[:], T.on2[:])
-        op("v", "ms", "", "LIM", T.LIM[:], 18.5)
-        op("v", "ms", "", "CB", T.CB[:], -1700.0)
-
-    def consts_d():
-        op("v", "ms", "", "onb", T.ONS[:], 1.0 / 2048.0)
-        op("v", "ms", "", "MK", T.MK[:], 1.0)
-        for ii in range(NB):
-            vts("J16 qm MK", "MKs", T.MK[:, STARTS[ii]:STARTS[ii] + 16], T.J16[:, 0:16], T.qm[:], O.is_gt, par=True)
-        vts("MKs MK", "MB", T.MB[:], T.MK[:], -1.0e8, O.mult, 1.0e8, O.add)
-
-    XW = "X X2"
-    Xw = T.X[:, 0:W]
-    CNw = T.CN[:, 0:U]
-    CH = [(0, 64), (64, 128), (128, 192)]
-    XG2 = "Xg2.0 Xg2.1 Xg2.2"
-    D2 = [("PA", T.PA), ("PB", T.PB), ("PA", T.PA)]
-    CNT = [("PB", T.PB, 0), ("PB", T.PB, 64), ("PC", T.PC, 0)]
-
-    def replay_rows(t):
-        mm("RSL%d TR0 TR1" % t, "PW", T.PW[:, 0:192], T.RSL[:, 128 * t:128 * t + 128], T.TR[:], True, True)
-        mm("IDh TR0 TR1", "PC", T.PC[:, 192:384], T.IDh[:], T.TR[:], True, True)
-        act("PC", "TRf", T.TRf[:], T.PC[:, 192:384], AF.Copy, bias=float(CMID))
-
-    def trail_a(j):
-        lo, hi = ((0, 128), (128, 192))[j]
-        vtt("sm%d PW" % j, "tD%d" % j, T.tD[:, lo:hi], T.sm[:, lo:hi], T.PW[:, 256 + lo:256 + hi], O.mult)
-
-    def trail_b(j, out, nm):
-        lo, hi = ((0, 128), (128, 192))[j]
-        vtt("tD%d PK" % j, nm + "%d" % j, out[:, lo:hi], T.PK[:, 192 + lo:192 + hi], T.tD[:, lo:hi], O.subtract)
-
-    def g2(c):
-        act(XW + " TRu%d" % (c // 2), "Xg2.%d" % c, T.Xg2[:, 1024 * c:1024 * c + 1024], Xw.indirect(T.TRu[:, 64 * c:64 * c + 64]))
-
-    def diff(c, Zk, k0=0, k1=16):
-        nm, P = D2[c]
-        for k in range(k0, k1):
-            mm("IDb " + Zk, nm, P[:, 64 * k:64 * k + 64], T.IDb[:], T[Zk][:, 64 * c:64 * c + 64], True, False)
-            mm("NIb Xg2.%d" % c, nm, P[:, 64 * k:64 * k + 64], T.NIb[:], T.Xg2[:, 1024 * c + k:1024 * c + 1024:16], False, True)
-
-    def absd(c):
-        nm, P = D2[c]
-        act(nm, "A2.%d" % c, T.A2[:, c, :], P[:], AF.Abs)
-
-    def thr(c):
-        vts("A2.%d LIM" % c, "IND.%d" % c, T.IND[:, c, :], T.A2[:, c, :], T.LIM[:], O.is_gt)
-
-    def count(c):
-        nm, P, o = CNT[c]
-        for k in range(16):
-            mm("PD1 IND.%d" % c, nm, P[:, o:o + 64], T.PD1[:, 15 - k:143 - k], T.IND[:, c, 64 * k:64 * k + 64], k == 0, k == 15)
-
-    def ttmax(c, fill=()):
-        lo, hi = CH[c]
-        for k in range(16):
-            vtt("Xg1.%d PZ" % c, "M1.%d" % c, T.M1[:, 4 * c:4 * c + 4, k::16], T.Xg1[:, 1024 * c + k:1024 * c + 1024:16],
-                T.PZ[:, lo:hi], O.max, par=True)
-            if k % 4 == 3 and k // 4 < len(fill):
-                fill[k // 4]()
-
-    def score(c):
-        lo, hi = CH[c]
-        for p in range(16):
-            mm("PDN M1.%d" % c, "PK", T.PK[:, lo:hi], T.PDN[:, 15 - p:143 - p], T.M1[:, 4 * c:4 * c + 4, 16 * p:16 * p + 16],
-               False, c == 2 and p == 15)
-
+    Xw, CNw, Z = T.X[:, 0:W], T.CN[:, 0:U], T.Z[:, 0:B]
+    DIFF = [("@A", T.PA), ("@B", T.PB), ("@A", T.PA)]
+    XG = "xw"
     outs = []
 
-    def fin(j):
-        c0 = 1536 * j
-        if j:
-            act(XW, "xo1", T.xraw[:, c0:c0 + 1536], T.X[:, c0:c0 + 1536], AF.Copy, bias=-float(XB))
-        else:
-            vts(XW, "xo0", T.xraw[:, c0:c0 + 1536], T.X[:, c0:c0 + 1536], -float(XB), O.add)
-        q = "sa"[j]
-        outs.append((q, dma(q, "xo%d" % j, "yx%d" % j, T.yx[:, c0:c0 + 1536], T.xraw[:, c0:c0 + 1536])))
-
-    for t in range(T_STEPS):
-        r = ROWS[t]
-        last = t == T_STEPS - 1
-        Zk, Zn = "Z%d" % t, "Z%d" % (t + 1)
-        Z = T[Zk]
-        vtc("CN VH", "Ku", T.Ku[:], CNw.indirect(T.VH[:]))
-        act("CN VH", "Kf", T.Kf[:], CNw.indirect(T.VH[:]), AF.Copy, bias=-float(CMID))
-        for c in (1, 2):
-            act(XW + " Ku", "Xg1.%d" % c, T.Xg1[:, 1024 * c:1024 * c + 1024], Xw.indirect(T.Ku[:, 64 * c:64 * c + 64]))
-        vtc(XW + " Ku", "Xg1.0", T.Xg1[:, 0:1024], Xw.indirect(T.Ku[:, 0:64]))
-        if not t:
-            consts_a()
-            mm("IDb " + Zk, "PZ", T.PZ[:, 0:192], T.IDb[:], Z[:], True, True)
-        else:
-            vtc("Sa", "Si", T.Si[:], T.Sa[:])
-            trail_a(1)
-            vts("Si", "Sj", T.Sj[:], T.Si[:], 3, O.bitwise_and)
-            trail_b(1, T.TR[:], "TR")
-            vts("Sj", "LIM", T.LIM[:], T.Sj[:], 18.5, O.add)
-            trail_list(1)
-        replay_rows(t)
-        mm("BOb zero", "PK", T.PK[:, 0:192], T.BOb[:], T.zero[:], True, False)
-        ttmax(0)
-        score(0)
-        if not t:
-            consts_b()
-            for c in range(2):
-                g2(c)
-                diff(c, Zk)
-        absd(0)
-        g2(2)
-        absd(1)
-        fills = [
-            lambda: [vts("Kf", "Kp", T.Kp[:, :, 16 * q:16 * q + 16], T.Kf[:, 96 * q:96 * q + 96], -1.0, O.mult, par=True) for q in range(2)],
-            lambda: op("v", "tr", "Kp", "V", T.V[:], T.Kp[:]),
-            lambda: vtt("PW DM", "WD", T.WD[:], T.PW[:, 0:192], T.DM[:], O.mult),
-            lambda: op("v", "scan", "A0 WD", "WS", T.WS[:], T.A0[:], T.WD[:], 0.0, O.mult, O.add),
-            lambda: vts("WS", "wi", T.wu[:, 0:12], T.WS[:, 15::16], float(CMID), O.add),
-            lambda: vts("wi", "ui", T.wu[:, 12:24], T.wu[:, 0:12], 1, O.arith_shift_right),
-            lambda: vtc("ui", "LU", T.LU[:], T.wu[:, 12:24]),
-            lambda: vts("ui", "wb", T.wb[:], T.wu[:, 12:24], -2.0, O.mult, float(CMID) - 0.5, O.add)]
-        ttmax(1, fills[:4])
+    def unturn(R, bank, P, c0, n, part, S="SWP"):
         for q in range(2):
-            for h in range(2):
-                mm("V " + SWPS, "PK", T.PK[:, 96 * q:96 * q + 96], T.SWP[:, 256 * h + 128 * q:256 * h + 128 * q + 128],
-                   T.V[:, :, 16 * h:16 * h + 16], False, False)
-        score(1)
-        ttmax(2, fills[4:])
-        score(2)
-        diff(2, Zk, 0, 8)
-        if not t:
-            consts_c()
-        thr(0)
-        count(0)
-        op("v", "scan", "RST PK", "Sc", T.Sc[:], T.RST[:], T.PK[:, 0:192], 0.0, O.max, O.min)
-        act("CN LU", "Co", T.Co[:], CNw.indirect(T.LU[:]), AF.Copy, bias=-float(CMID))
-        vts("Sc", "ci", T.ci[:], T.Sc[:, 15::16], float(CMID), O.add)
-        vts("ci", "cm", T.cm[:], T.ci[:], 4095, O.bitwise_and)
-        vts("cm", "cf", T.cf[:], T.cm[:], -float(CMID), O.add)
-        vtc("cm", "CL", T.CL[:], T.cm[:])
-        if not last:
-            vts("cm", "ch", T.ch[:], T.cm[:], 1, O.arith_shift_right)
-        vtt("cf RP DM", "Dg", T.Dg[:], T.cf[:].indirect(T.RP[:]), T.DM[:], O.mult)
-        if not last:
-            vtt(XW + " CL " + Zk, "sg", T.sg[:], Xw.indirect(T.CL[:]), Z[:], O.add)
-        mm("BOh Dg", "PZ", T.PZ[:, 192:384], T.BOh[:], T.Dg[:], True, True)
-        mm("IDm%d TR0 TR1" % t, "PK", T.PK[:, 192:384], T.IDm[:, 128 * t:128 * t + 128], T.TR[:], True, False)
-        mm("PDH Dg", "PK", T.PK[:, 192:384], T.PDH[:, 15 - t:143 - t], T.Dg[:], False, True)
-        if not last:
-            vtc("ch", "VH", T.VH[:], T.ch[:])
-            vts("sg", "ZN%d" % t, T["ZN%d" % t][:], T.sg[:], 0.5, O.mult, -0.25, O.add)
+            mms(bank, P[:, c0 + q:c0 + n:2], [(R + " " + S, T[S][:, 256 * h + 128 * q:256 * h + 128 * q + 128], part(h)) for h in range(2)])
+
+    def turn(R, Wr, o, i, **k):
+        op("v", "tr", R, Wr, o, i, **k)
+
+    FW = NB * RUN
+    FE = slice(RUN - 1, FW, RUN)
+
+    def calls(t):
+        r, last = ROWS[t], t == T_STEPS - 1
+        ks = [k for k in range(16) if k != r]
+        xw = T.xw[:]
+        lim, hm, nhm = "LIM%d" % t, T.HM[:, t, :], T.NHM[:, t, :]
+        c = {}
+        c["wt"] = lambda: turn("TR", "Wt", T.Wt[:], T.TR[:])
+        c["wl"] = lambda: unturn("Wt", "@U:w", T.PU, 384, NB, lambda h: T.Wt[:, 16 * h + r::32])
+        c["lu"] = lambda: vts("@U:w", "LU", T.LU[:], T.PU[:, 384:384 + NB], CMID - 0.5, O.add, 0.5, O.mult)
+        c["lw"] = lambda: vts("@U:w", "LW", T.LW[:], T.PU[:, 384:384 + NB], float(CMID), O.add)
+        c["xw"] = lambda: act(XW + " LW", "xw", xw, Xw.indirect(T.LW[:]))
+        c["wf"] = lambda: act("@U:w", "wf", T.wf[:], T.PU[:, 384:384 + NB])
+        c["ulf"] = lambda: vts("LU", "ul", T.ul[:], T.LU[:], -float(CMID), O.add)
+        c["urow"] = lambda: act(IO + " LU", "urow", T.urow[:], T.IOTA[:].indirect(T.LU[:]))
+        c["co"] = lambda: act(CW + " LU", "Co", T.Co[:], CNw.indirect(T.LU[:]), AF.Copy, bias=-float(CMID))
+        c["pd"] = lambda: mms("@U:d", T.PU[:, 0:B], [("NID TR", T.NID[:], T.TR[:]), ("ID Co", T.ID[:], T.Co[:])])
+        c["mid"] = lambda: act("TR", "Mid", T.Mid[:], T.TR[:], AF.Copy, bias=float(CMID))
+        for j in range(4):
+            c["cn%d" % j] = lambda j=j: vtc("craw%d" % j, "CN%d" % j, T.CN[:, 384 * j:384 * j + 384], T.craw[:, 384 * j:384 * j + 384])
+
+        c["kr"] = lambda: act(CW + " VH", "Kh", T.Kh[:], CNw.indirect(T.VH[:]), AF.Copy, bias=-float(CMID))
+        c["kt"] = lambda: [turn("Kh", "V", T.V[:, :, i], T.Kh[:, 32 * i:32 * i + 32], par=True) for i in range(6)]
+        c["kl"] = lambda: unturn("V", "@F:k", T.PF, 256, B, lambda h: T.V[:, 16 * h:16 * h + 16, :])
+        c["ko"] = lambda: vts("@F:k", "KT", T.KT[:], T.PF[:, 256:256 + B], float(CMID), O.add)
+        c["za"] = lambda: vts("ZI%d" % t, "Za", Z, T["ZI%d" % t][:], -float(XB), O.add)
+        c["zb"] = lambda: vts("ZI%d" % t, "Zb", T.Z[:, B:2 * B], T["ZI%d" % t][:], -float(XB), O.add)
+
+        def score(j):
+            if not j:
+                mm("ID Kh", "@K", T.PK[:, 0:B], T.ID[:], T.Kh[:], True, False)
+            for k in (2 * j, 2 * j + 1):
+                mm("PDN M%d" % j, "@K", T.PK[:, 0:B], T.PDN[:, 15 - k:143 - k], T.M[:, j, B * (k % 2):B * (k % 2) + B], False, k == 15)
+
+        for j in range(8):
+            c["mx%d" % j] = lambda j=j: vtt(XW + " KT Za Zb", "M%d" % j, T.M[:, j, :], Xw.indirect(T.KT[:, 24 * j:24 * j + 24]), T.Z[:], O.max)
+            c["s%d" % j] = lambda j=j: score(j)
+        c["tp"] = lambda: turn("@K", "key", T.key[:], T.PK[:, 0:B])
+        c["sc"] = lambda: scan("RST key", "Sc", T.Sc[:], T.RST[:], T.key[:], O.max, O.min)
+        c["ci"] = lambda: vts("Sc", "ci", T.ci[:], T.Sc[:, 15::16], GRID, O.add, GRID, O.subtract)
+        c["cm"] = lambda: vtt("Sc ci", "cm", T.cm[:], T.Sc[:, 15::16], T.ci[:], O.subtract)
+        c["cw"] = lambda: unturn("cm", "@U:c", T.PU, 448, NB, lambda h: T.cm[:, h::2])
+        c["cl"] = lambda: vts("@U:c", "CL", T.CL[:], T.PU[:, 448:448 + NB], float(CMID), O.add)
+        c["cf"] = lambda: vtc("@U:c", "cf", T.cf[:], T.PU[:, 448:448 + NB])
+        c["crow"] = lambda: act(IO + " CL", "crow", T.crow[:], T.IOTA[:].indirect(T.CL[:]))
+        c["xc"] = lambda: act(XW + " CL", "xc", T.xc[:], Xw.indirect(T.CL[:]))
+        c["xcut"] = lambda: act("xc", "xcut", T.xcut[:], T.xc[:], AF.Copy, scale=0.5, bias=XB - 0.25)
+
+        def diff(i, h):
+            bank, P = DIFF[i]
+            for s in range(8 * h, min(8 * h + 8, 15)):
+                mms(bank + str(h), P[:, 64 * s:64 * s + 64],
+                    [("NID Xg%d" % i, T.NID[:], T.Xg[:, 1024 * i + ks[s]:1024 * i + 1024:16]), ("ID Za", T.ID[:], T.Z[:, 64 * i:64 * i + 64])])
+
+        def thr(i):
+            if i in ON_SCALAR:
+                act("A%d N%s" % (i, lim), "IND%d" % i, T.IND[:, i, :], T.A2[:, i, :], AF.Sigmoid, scale=STEEP, bias=T.NLIM[:, t:t + 1])
+            else:
+                vts("A%d %s" % (i, lim), "IND%d" % i, T.IND[:, i, :], T.A2[:, i, :], T.LIM[:, t:t + 1], O.is_gt)
+
+        def count(i):
+            mms("@C:n%d" % i, T.PC[:, 64 * i:64 * i + 64],
+                [("PD1 IR", T.PD1[:, 15 - r:143 - r], T.IR[:, 64 * i:64 * i + 64])] +
+                [("PD1 IND%d" % i, T.PD1[:, 15 - k:143 - k], T.IND[:, i, 64 * s:64 * s + 64]) for s, k in enumerate(ks)])
+
+        for i in range(3):
+            bank, P = DIFF[i]
+            c["g%d" % i] = lambda i=i: act(XW + " TRu", "Xg%d" % i, T.Xg[:, 1024 * i:1024 * i + 1024], Xw.indirect(T.TRu[:, 64 * i:64 * i + 64]))
+            c["d%da" % i] = lambda i=i: diff(i, 0)
+            c["d%db" % i] = lambda i=i: diff(i, 1)
+            c["ab%d" % i] = lambda i=i, bank=bank, P=P: act("%s0 %s1" % (bank, bank), "A%d" % i, T.A2[:, i, :], P[:, 0:960], AF.Abs)
+            c["th%d" % i] = lambda i=i: thr(i)
+            c["n%d" % i] = lambda i=i: count(i)
+        c["dr"] = lambda: mms("@C:r", T.PC[:, B:2 * B], [("ID Za", T.ID[:], Z), ("NID " + XG, T.NID[:], xw)])
+        c["ar"] = lambda: act("@C:r", "AR", T.AR[:], T.PC[:, B:2 * B], AF.Abs)
+        c["ir"] = lambda: vts("AR " + lim, "IR", T.IR[:], T.AR[:], T.LIM[:, t:t + 1], O.is_gt)
+        c["br"] = lambda: mm("BO IR", "@C:r", T.PC[:, B:2 * B], T.BO[:], T.IR[:], True, True)
+        nine = dict(scale=STEEP, bias=-8.5 * STEEP)
+        if last:
+            c["sr"] = lambda: act("@C:r", "sr", T.sr[:], T.PC[:, B:2 * B], AF.Sigmoid, **nine)
+        else:
+            c["sr"] = lambda: act("@C:r", "sr Sa", T.sr[:], T.PC[:, B:2 * B], AF.Sigmoid, accum_out=T.Sa[:], **nine)
+        c["sev"] = lambda: act("@C:n0 @C:n1 @C:n2", "sev", T.sev[:], T.PC[:, 0:B], AF.Sigmoid, **nine)
+
+        def fold(E, own):
+            mm("ID NM", "@F", T.PF[:, 0:FW], T.ID[:], T.NM[:], True, False)
+            mm("ID " + own, "@F", T.PF[:, 0:FW:RUN], T.ID[:], T[own][:], False, False)
+            for s in reversed(range(NB)):
+                nm = "I8" if s else "I4"
+                names = " ".join("%s%d" % (E, b) for b in range(s, NB))
+                mm(names + " %sz %s" % (E, nm), "@F", T.PF[:, RUN * s:FW], T[nm][:], T[E][:, s:NB, NB - 1 - s, :], False, s == 0)
+
+        for n, E, F, row, col, own in (("w", "Ew", "Fw", "urow", "ul", "wf"), ("c", "Ec", "Fc", "crow", "cf", "cf")):
+            for b in range(NB):
+                c["e%s%d" % (n, b)] = lambda b=b, E=E, row=row, col=col: vts(
+                    row + " " + col, "%s%d" % (E, b), T[E][:, b, NB - 1 - b:NB, 1:17], T[row][:, 0:16 * b + 16], T[col][:, b:b + 1], O.is_equal)
+            c["fo" + n] = lambda E=E, own=own: fold(E, own)
+            c["f" + n] = lambda F=F: scan("RS @F", F, T[F][:], T.RS[:], T.PF[:, 0:FW], O.min, O.max)
+        c["lh"] = lambda: vts("Fw", "LH", T.LH[:], T.Fw[:, FE], float(CMID), O.add)
+        c["st"] = lambda: turn("sr", "St", T.St[:], T.sr[:])
+        c["sk"] = lambda: unturn("St", "@U:s", T.PU, 256, NB, lambda h: T.St[:, 16 * h::32], "SW4")
+        c["lcf"] = lambda: vtt("@U:s Fw", "LCf", T.LCf[:], T.PU[:, 256:256 + NB], T.Fw[:, FE], O.add)
+        c["lc"] = lambda: vts("LCf", "LC", T.LC[:], T.LCf[:], CMID - 0.5, O.add, 0.5, O.mult)
+        c["ul"] = lambda: vts("Fc", "UL", T.UL[:], T.Fc[:, FE], float(CMID), O.add)
+
+        c["p1"] = lambda: mms("@C:r", T.PC[:, B:2 * B], [("NHI " + XG, T.NHI[:], xw), ("NHI Za", T.NHI[:], Z), ("I512 sr", T.I512[:], T.sr[:])])
+        c["p2"] = lambda: mms("@F:k", T.PF[:, 256:256 + B], [("ID " + XG, T.ID[:], xw), ("ID c508", T.ID[:], T.c508[:]), ("I512 sr", T.I512[:], T.sr[:])])
+        c["t1"] = lambda: act("@C:r", "t1", T.t1[:], T.PC[:, B:2 * B], AF.Relu, scale=-1.0, bias=XB - 0.25)
+        c["t2"] = lambda: vts("@F:k", "t2", T.t2[:], T.PF[:, 256:256 + B], 63.0, O.min, -float(XB), O.max)
+        c["xr"] = lambda: vtt("t1 t2 LH", XW, T.X[:].indirect(T.LH[:]), T.t1[:], T.t2[:], O.add)
+        c["xk"] = lambda: vtt("xcut cxb UL", XW, T.X[:].indirect(T.UL[:]), T.xcut[:], T.cxb[:], O.add)
+
+        c["q1"] = lambda: mms("@B0", T.PB[:, 0:B], [("HM%d Kh" % t, hm, T.Kh[:]), ("NHM%d TR" % t, nhm, T.TR[:])])
+        c["q2"] = lambda: mms("@B1", T.PB[:, 512:512 + B], [("HM%d TR" % t, hm, T.TR[:]), ("PDS crow", T.PDS[:, 15 - t:143 - t], T.crow[:])] +
+                              ([("ID cmid", T.ID[:], T.cmid[:])] if last else []))
+        c["cd"] = lambda: vtt("@U:d sev", "cD", T.cD[:], T.PU[:, 0:B], T.sev[:], O.mult)
+        c["td"] = lambda: vtt("@B0 sev", "tD", T.tD[:], T.PB[:, 0:B], T.sev[:], O.mult)
+        c["cs"] = lambda: vtt("cD Mid LC", CW, T.CN[:].indirect(T.LC[:]), T.cD[:], T.Mid[:], O.add)
+
+        def store(R, name, o, i, n):
+            w = o.shape[1] // n
+            for j in range(n):
+                outs.append(dma("s", R, "%s%d" % (name, j), o[:, w * j:w * j + w], i[:, w * j:w * j + w]))
+
+        if last:
+            c["tr"] = lambda: vtt("@B1 tD", "TF", T.TF[:], T.PB[:, 512:512 + B], T.tD[:], O.add)
+            c["ox"] = lambda: store(XW, "yx", T.yx, T.X, 2)
+            c["ol"] = lambda: store(CW, "yl", T.yl, T.CN, 2)
+            c["og"] = lambda: store("TF", "yg", T.yg, T.TF, 1)
+            return c
+        c["tr"] = lambda: vtt("@B1 tD", "TR", T.TR[:], T.PB[:, 512:512 + B], T.tD[:], O.add)
+        c["tru"] = lambda: vts("TR", "TRu", T.TRu[:], T.TR[:], float(CMID), O.add)
+        c["vh"] = lambda: vts("@U:c", "VH", T.VH[:], T.PU[:, 448:448 + NB], CMID - 0.5, O.add, 0.5, O.mult)
+        c["sa"] = lambda: mm("ONf Sa", "@U:a", T.PU[:, 320:321], T.ONf[:], T.Sa[:], True, True)
+        c["si"] = lambda: vtc("@U:a", "Si", T.Si[:], T.PU[:, 320:321])
+        c["sj"] = lambda: vts("Si", "Sj", T.Sj[:], T.Si[:], 3, O.bitwise_and)
+        c["lim"] = lambda: vts("Sj", "LIM%d" % (t + 1), T.LIM[:, t + 1:t + 2], T.Sj[:], 18.5, O.add)
+        c["nlim"] = lambda: vts("Sj", "NLIM%d" % (t + 1), T.NLIM[:, t + 1:t + 2], T.Sj[:], 18.5, O.add, -STEEP, O.mult)
+        zo, zi = "ZO%d" % (t + 1), "ZI%d" % (t + 1)
+        c["gs"] = lambda: mms("@K", T.PK[:, B:2 * B], [("ID Za", T.ID[:], Z), ("ID xc", T.ID[:], T.xc[:])])
+        c["zn"] = lambda: act("@K", zo, T[zo][:], T.PK[:, B:2 * B], AF.Copy, scale=0.5, bias=XB - 0.25)
+
+        def send():
             dst = T.cores[(rank + 1 + t % (N - 1)) % N]
             rid, pid, _e = topo.addr(dst)
-            need("g", wr["ZN%d" % t][0], wr["ZN%d" % t][1])
-            g.remote_dma(T[Zn][:], T["ZN%d" % t][:], T.sem["zs%d" % (t + 1)], T.sem.zsent, pid, rid, topo.mask(core, dst))
+            need("g", wr[zo][0], wr[zo][1])
+            g.remote_dma(T[zi][:], T[zo][:], T.sem["zs%d" % (t + 1)], T.sem.zsent, pid, rid, topo.mask(core, dst))
             src = T.cores[(rank - 1 - t % (N - 1)) % N]
-            note("zs%d" % (t + 1), len(topo.engines(src, core)), [], [Zn])
-        vtt("Co PC", "CG", T.CG[:], T.Co[:], T.PC[:, 192:384], O.subtract)
-        mm("IDb " + Zk, "PK", T.PK[:, 0:192], T.IDb[:], Z[:], True, False)
-        mm("NIb " + XG2, "PK", T.PK[:, 0:192], T.NIb[:], T.Xg2[:, r::16], False, True)
-        act("PK", "AR", T.AR[:], T.PK[:, 0:192], AF.Abs)
-        if not t:
-            consts_d()
-        vtc("PZ", "ACh", T.ACh[:], T.PZ[:, 192:384])
-        for ii in range(NB):
-            vts("ACh cf", "E", T.E[:, STARTS[ii]:STARTS[ii + 1]], T.ACh[:, 16 * ii:192], T.cf[:, ii:ii + 1], O.is_equal, par=True)
-        mm("IDb " + XG2, "PZ", T.PZ[:, 192:384], T.IDb[:], T.Xg2[:, r::16], True, False)
-        mm("IDb " + Zk, "PZ", T.PZ[:, 192:384], T.IDb[:], Z[:], False, True)
-        diff(2, Zk, 8, 16)
-        act("PZ", "H", T.H[:], T.PZ[:, 192:384], AF.Copy, scale=0.5, bias=-0.25)
-        for ii in range(NB):
-            act("PW wb", "SQ", T.SQ[:, STARTS[ii]:STARTS[ii + 1]], T.PW[:, 16 * ii:192], AF.Square, bias=T.wb[:, ii:ii + 1], par=True)
-        vts("AR LIM", "IR", T.IR[:], T.AR[:], T.LIM[:], O.is_gt)
-        vts(XG2, "Q", T.Q[:], T.Xg2[:, r::16], 4.0, O.add, XB + 63.0, O.min)
-        mm("BOb IR", "PC", T.PC[:, 192:384], T.BOb[:], T.IR[:], True, True)
-        for p in range(16):
-            mm("PD1 IR", "PC", T.PC[:, 384:396], T.PD1[:, 15 - p:143 - p], T.IR[:, p::16], p == 0, p == 15)
-        mm("IDb Q", "PZ", T.PZ[:, 0:192], T.IDb[:], T.Q[:], True, False)
-        mm("NIb H", "PZ", T.PZ[:, 0:192], T.NIb[:], T.H[:], False, True)
-        act(XW + " CL", "xcut", T.xcut[:], Xw.indirect(T.CL[:]), AF.Copy, scale=0.5, bias=XB / 2 - 0.25)
-        act("PC CB", "skr", T.skr[:], T.PC[:, 192:384], AF.Sigmoid, bias=T.CB[:], scale=200.0)
-        absd(2)
-        act("LIM", "LB", T.LB[:], T.LIM[:], AF.Copy, scale=-200.0)
-        act("A2.2 LB", "IND.2", T.IND[:, 2, :], T.A2[:, 2, :], AF.Sigmoid, bias=T.LB[:], scale=200.0)
-        op("v", "scan", "E MK MKs", "EC", T.EC[:], T.E[:], T.MK[:], 0.0, O.max, O.mult)
-        thr(1)
-        count(1)
-        for q in range(2):
-            mm("IDm%d Kp" % t, "PW", T.PW[:, 256 + 96 * q:352 + 96 * q], T.IDm[:, 128 * t:128 * t + 128], T.Kp[:, :, 16 * q:16 * q + 16], True, False)
-            mm("IDm%d TR0 TR1" % t, "PW", T.PW[:, 256 + 96 * q:352 + 96 * q], T.IDm[:, 128 * t:128 * t + 128], T.TR[:, 96 * q:96 * q + 96], False, True)
-        op("v", "scan", "SQ MB", "SW", T.SW[:], T.SQ[:], T.MB[:], 1.0e8, O.min, O.max)
-        vtt("EC ENDS DUM", "ULf", T.ULf[:], T.EC[:].indirect(T.ENDS[:, 0:1]), T.DUM[:, 0:16], O.mult)
-        vts("SW ENDS", "NF", T.NF[:], T.SW[:].indirect(T.ENDS[:]), 1.0, O.is_lt)
-        vtt("ULf cm", "ULg", T.ULf[:, 0:12], T.ULf[:, 0:12], T.cm[:], O.max)
-        vtt("NF DUM", "e1", T.e1[:], T.NF[:, 0:24], T.DUM[:, 0:24], O.mult)
-        vtc("ULg", "UL", T.UL[:], T.ULf[:, 0:12])
-        vtt("e1 wi ui", "WU", T.WU[:], T.e1[:], T.wu[:], O.max)
-        vts("PC", "skb", T.skb[:], T.PC[:, 384:396], 8.5, O.is_gt, 2048.0, O.mult)
-        vtc("WU", "LH", T.LH[:], T.WU[:, 0:12])
-        vtt("skr PZ", "mQ", T.mQ[:], T.skr[:], T.PZ[:, 0:192], O.mult)
-        vtt("skb WU", "LCf", T.LCf[:], T.skb[:], T.WU[:, 12:24], O.add)
-        vts("PB", "sm0", T.sm[:, 0:128], T.PB[:, 0:128], 8.5, O.is_gt)
-        vtt("mQ H LH", XW, T.X[:].indirect(T.LH[:]), T.mQ[:], T.H[:], O.add)
-        vtc("LCf", "LC", T.LC[:], T.LCf[:])
-        if not last:
-            trail_a(0)
-        vtc("xcut UL", XW, T.X[:].indirect(T.UL[:]), T.xcut[:])
-        if last:
-            for j in range(2):
-                fin(j)
-        if not last:
-            mm("onb skb", "PC", T.PC[:, 400:412], T.ONS[:], T.skb[:], True, True)
-            act("PC", "jnk Sa", T.jnk[:], T.PC[:, 400:412], AF.Copy, accum_out=T.Sa[:])
-        count(2)
-        if not last:
-            trail_b(0, T.TR[:], "TR")
-        vtt("sm0 CG", "cD0", T.cD[:, 0:128], T.sm[:, 0:128], T.CG[:, 0:128], O.mult)
-        if not last:
-            trail_list(0)
-            for c in range(2):
-                g2(c)
-            mm("IDb " + Zn, "PZ", T.PZ[:, 0:192], T.IDb[:], T[Zn][:], True, True)
-            diff(0, Zn)
-        vtt("cD0 TRf LC", "CN", T.CN[:].indirect(T.LC[:, 0:8]), T.cD[:, 0:128], T.TRf[:, 0:128], O.add)
-        vts("PC", "sm1", T.sm[:, 128:192], T.PC[:, 0:64], 8.5, O.is_gt)
-        vtt("sm1 CG", "cD1", T.cD[:, 128:192], T.sm[:, 128:192], T.CG[:, 128:192], O.mult)
-        vtt("cD1 TRf LC", "CN", T.CN[:].indirect(T.LC[:, 8:12]), T.cD[:, 128:192], T.TRf[:, 128:192], O.add)
-        if not last:
-            diff(1, Zn)
-    for j in range(2):
-        q = "sa"[j]
-        outs.append((q, dma(q, "CN", "yl%d" % j, T.yl[:, 768 * j:768 * j + 768], T.CN[:, 768 * j:768 * j + 768])))
-    for j in range(2):
-        trail_a(j)
-        trail_b(j, T.TF[:], "TF")
-    vts("TF0 TF1 REV", "go", T.sg[:], T.TF[:].indirect(T.REV[:]), float(CMID), O.add)
-    outs.append(("s", dma("s", "go", "yg", T.yg[:], T.sg[:])))
-    for q, s in outs:
-        need(q, s, 16)
+            note("zs%d" % (t + 1), len(topo.engines(src, core)), [], [zi])
+
+        c["send"] = send
+        return c
+
+    C = [calls(t) for t in range(T_STEPS)] + [{}]
+    for name in FIRST.split():
+        C[0][name]()
+    for t in range(T_STEPS):
+        for name in STEP.split():
+            c = C[t + 1] if name[0] == "+" else C[t]
+            if name.strip("+") in c:
+                c[name.strip("+")]()
+    for s in outs:
+        need("s", s, 16)
     g.wait_ge(T.sem.zsent, sum(len(topo.engines(core, T.cores[(rank + 1 + t % (N - 1)) % N])) for t in range(T_STEPS - 1)))

from concourse.mybir import dt, AluOpType, AxisListType, ActivationFunctionType

W, U, B, T_STEPS = 3072, 1536, 192, 7
NB = B // 16
CMID = 1536
XB = 192
ROWS = [(t + 13) % 16 for t in range(T_STEPS)]
BIG = 1.0e6
RUN = 18
ON_SCALAR = (0,)
STEEP = 256.0
GRID = 1.5 * 2.0 ** 35

f32, b16, f16, i32, u16 = "float32", "bfloat16", "float16", "int32", "uint16"
_S = {
    "X": ([128, W + 2 * B], b16), "CN": ([128, 3840], f32), "TR": ([128, B], f16), "TRu": ([128, B], u16),
    "craw": ([128, U], i32), "traw": ([128, B], i32), "vraw": ([128, B], i32), "vh": ([128, B], f16),
    "Z": ([128, 2 * B], b16), "Kh": ([128, B], f16), "V": ([128, 32, 6], f16), "KT": ([128, B], u16),
    "M": ([128, 8, 2 * B], b16), "key": ([128, B], f32), "Sc": ([128, B], f32), "RST": ([128, B], f32),
    "Wt": ([128, B], f16), "St": ([128, B], b16),
    "Xg": ([128, W], b16), "A2": ([128, 3, 960], b16), "IND": ([128, 3, 960], b16),
    "AR": ([128, B], b16), "IR": ([128, B], b16), "sr": ([128, B], b16), "sev": ([128, B], b16), "Sa": ([128, 1], f32),
    "ci": ([128, NB], f32), "cm": ([128, NB], f16), "cf": ([128, NB], f16),
    "CL": ([128, NB], u16), "VH": ([128, NB], u16), "UL": ([128, NB], u16), "LU": ([128, NB], u16), "LH": ([128, NB], u16),
    "LC": ([128, NB], u16), "LCf": ([128, NB], f32), "ul": ([128, NB], f32), "wf": ([128, NB], f16),
    "crow": ([128, B], f16), "urow": ([128, B], f16), "Co": ([128, B], f16),
    "Ew": ([128, NB, NB, RUN], b16), "Ec": ([128, NB, NB, RUN], b16), "Fw": ([128, NB * RUN], f32), "Fc": ([128, NB * RUN], f32),
    "xw": ([128, B], b16), "LW": ([128, NB], u16), "xc": ([128, B], b16), "xcut": ([128, B], b16),
    "t1": ([128, B], b16), "t2": ([128, B], b16), "Mid": ([128, B], f32), "cD": ([128, B], f32), "tD": ([128, B], f32), "TF": ([128, B], f32),
    "Si": ([128, 1], i32), "Sj": ([128, 1], i32), "LIM": ([128, 8], f32), "NLIM": ([128, 8], f32),
    "IOTA": ([128, W], f32), "qi": ([128, 1], i32), "qa": ([128, 1], i32), "qm": ([128, 1], f32), "half": ([128, 2], f32),
    "J16": ([128, 16], f32), "lane": ([128, NB], f32), "RS": ([128, NB * RUN], f32), "NM": ([128, NB * RUN], b16),
    "on": ([128, 144], f32), "on2": ([128, 144], f32), "BOf": ([128, 128], f32), "IDf": ([128, 128], f32),
    "sh0": ([128, 128], f32), "sh1": ([128, 128], f32), "ONf": ([128, 128], f32), "SWP": ([128, 512], b16), "BO": ([128, 128], b16),
    "PD1": ([128, 144], b16), "PDN": ([128, 144], b16), "PDS": ([128, 144], b16), "PDC": ([128, 144], b16),
    "SW4": ([128, 512], b16), "HM": ([128, T_STEPS, 128], b16), "NHM": ([128, T_STEPS, 128], b16),
    "cmid": ([128, B], b16), "cxb": ([128, B], b16), "c508": ([128, B], b16),
}
IDS = {"ID": 1.0, "NID": -1.0, "NHI": -0.5, "I512": 512.0, "I4": 4096.0, "I8": 8192.0}
for _k in IDS:
    _S[_k] = ([128, 128], b16)
for _t in range(1, T_STEPS):
    _S["ZI%d" % _t] = ([128, B], b16)
    _S["ZO%d" % _t] = ([128, B], b16)
SCRATCH = {k: ("sbuf", s, d) for k, (s, d) in _S.items()}
SCRATCH.update({
    "PA": ("psum", [128, 1024], f32), "PB": ("psum", [128, 1024], f32), "PK": ("psum", [128, 512], f32),
    "PF": ("psum", [128, 512], f32), "PU": ("psum", [128, 512], f32), "PC": ("psum", [128, 512], f32),
})
SEMAPHORES = ["sv", "sp", "sa", "sg", "zsent"] + ["zs%d" % t for t in range(1, T_STEPS)] + ["d%d" % i for i in range(40)]

FIRST = "wt g0 cn0 wl cn1 cn2 cn3 lw mid kr kt kl ko"
STEP = """
d0a xw mx0 mx1 mx2 dr d0b mx3 mx4 s0 g1 ar g2 s1 ir d1a mx5 mx6 lu ab0 d1b s2 mx7 s3 s4 br s5 sr s6 ulf d2a urow
ew11 s7 ew10 ew9 ew8 ew7 tp ew6 sc ew5 wf th0 ci ew4 ew3 d2b p2 p1 cm ew2 t2 cw ab2 ew1 ew0 ab1 st vh cl
fow sk crow n0 th2 fw cf lcf lh n2 co sa lc xc gs t1 th1 n1 ec11 ec10 ec9 ec8 ec7 ec6 si ec5 pd zn ec4 ec3 q1 sev xcut ec2 send ec1 sj ec0
foc xr cd q2 td cs ol fc tr og ul tru xk ox nlim +kr +mid +kt +wt +za lim +kl +zb +wl +g0 +lw +ko
"""


def rank_program(g, core, T, topo):
    rank = T.rank_of(core)
    if rank is None:
        return
    O, AF = AluOpType, ActivationFunctionType
    N = len(T.cores)
    ENG = {"v": g.vector, "p": g.tensor, "a": g.scalar, "g": g, "s": g.sync}
    cnt, known, wr, rd = {}, {}, {}, {}

    def need(q, src, n):
        if known.get((q, src), 0) < n:
            known[(q, src)] = n
            ENG[q].wait_ge(T.sem[src], n)

    def keys(names):
        return [k.split(":")[0] for k in names.split()]

    def deps(q, R, Wr, par):
        own = "s" + q
        for k in R:
            if k in wr and not (q == "p" and wr[k][0] == own):
                need(q, wr[k][0], wr[k][1])
            if k[0] == "@":
                for s, n in rd.get(k, {}).items():
                    if s != own:
                        need(q, s, n)
        for k in Wr:
            if k in wr and not (wr[k][0] == own and (par or q == "p")):
                need(q, wr[k][0], wr[k][1])
            for s, n in rd.get(k, {}).items():
                if not (s == own and (par or q == "p")):
                    need(q, s, n)

    def note(src, n, R, Wr):
        for k in R:
            rd.setdefault(k, {})[src] = n
        for k in Wr:
            wr[k] = (src, n)
            rd[k] = {}

    def op(q, name, R, Wr, *a, par=False, **kw):
        R, Wr = keys(R), keys(Wr)
        deps(q, R, Wr, par)
        if q == "v":
            e = g.vector
            fn = {"tc": e.tensor_copy, "ts": e.tensor_scalar, "tt": e.tensor_tensor, "scan": e.tensor_tensor_scan,
                  "ms": e.memset, "tr": e.transpose}[name]
        elif q == "a":
            fn = g.scalar.activation
        elif q == "p":
            fn = g.tensor.matmul
        else:
            fn = {"iota": g.iota, "sel": g.affine_select}[name]
        src = "s" + q
        cnt[src] = cnt.get(src, 0) + 1
        fn(*a, **kw).then_inc(T.sem[src], 1)
        note(src, cnt[src], R, Wr)

    nd = [0]

    def dma(q, R, Wr, out, in_):
        R, Wr = keys(R), keys(Wr)
        deps(q, R, Wr, True)
        s = "d%d" % nd[0]
        nd[0] += 1
        ENG[q].dma_start(out, in_).then_inc(T.sem[s], 16)
        note(s, 16, R, Wr)
        return s

    def vtc(R, Wr, o, i, **k):
        op("v", "tc", R, Wr, o, i, **k)

    def vts(R, Wr, o, i, s1, o0, s2=None, o1=None, **k):
        if o1 is None:
            op("v", "ts", R, Wr, o, i, s1, None, o0, **k)
        else:
            op("v", "ts", R, Wr, o, i, s1, s2, o0, o1, **k)

    def vtt(R, Wr, o, a, b, f, **k):
        op("v", "tt", R, Wr, o, a, b, f, **k)

    def vms(Wr, o, c, **k):
        op("v", "ms", "", Wr, o, c, **k)

    def scan(R, Wr, o, a, b, o0, o1):
        op("v", "scan", R, Wr, o, a, b, 0.0, o0, o1)

    def act(R, Wr, o, i, f=AF.Copy, **k):
        op("a", "act", R, Wr, o, i, f, **k)

    def mm(R, Wr, o, l, r, st, sp):
        op("p", "mm", R, Wr, o, l, r, st, sp)

    def mms(bank, o, terms):
        for i, (R, l, r) in enumerate(terms):
            mm(R, bank, o, l, r, i == 0, i == len(terms) - 1)

    def sel(R, Wr, o, i, pat, cmp, base, mult):
        op("g", "sel", R, Wr, o, i, pat, cmp, 0.0, base, mult)

    def iota(Wr, o, pat, base, mult):
        op("g", "iota", "", Wr, o, pat, base, mult, allow_small_or_imprecise_dtypes=True)

    XW = "X0 X1 X2 X3"
    CW = "CN0 CN1 CN2 CN3"
    dma("s", "", "vraw", T.vraw[0:8, :], T.cut[:])
    dma("a", "", "traw", T.traw[:], T.trail[:])
    for j in range(4):
        dma("sa"[j % 2], "", "X%d" % j, T.X[:, 768 * j:768 * j + 768], T.x[:, 768 * j:768 * j + 768])
    dma("s", "", "Za", T.Z[:, 0:B], T.z[:])
    dma("a", "", "Zb", T.Z[:, B:2 * B], T.z[:])
    for j in range(4):
        dma("sa"[j % 2], "", "craw%d" % j, T.craw[:, 384 * j:384 * j + 384], T.canal[:, 384 * j:384 * j + 384])
    op("g", "iota", "", "qi", T.qi[:], [[1, 1]], 0, 1)
    iota("J16", T.J16[:], [[1, 16]], 0, 0)
    iota("lane", T.lane[:], [[32, NB]], W - CMID, 0)
    vms("on", T.on[:], 1.0)
    vms("fon", T.sh0[:], 1.0)
    vms("on2", T.on2[:], 0.0)
    vms("cmid", T.cmid[:], float(CMID))
    vms("RST", T.RST[:], -1.0e8)
    vms("on2", T.on2[:, 15::16], 1.0)
    vms("RST", T.RST[:, 0::16], 1.0e8)
    sel("fon", "IDf", T.IDf[:], T.sh0[:], [[-1, 128]], O.is_equal, 0, 1)
    sel("on", "PDC", T.PDC[0:8, :], T.on[0:8, :], [[1, 144]], O.is_equal, -15, -16)
    sel("fon", "sh1", T.sh1[:], T.sh0[:], [[-1, 128]], O.is_equal, -16, 1)
    sel("fon", "sh0", T.sh0[:], T.sh0[:], [[-1, 128]], O.is_equal, 16, 1)
    iota("IO0", T.IOTA[:, 0:768], [[1, 768]], -CMID, 0)
    sel("on2", "on2", T.on2[:], T.on2[:], [[-16, 9], [0, 16]], O.is_ge, 0, 1)
    sel("on", "on", T.on[:, 0:128], T.on[:, 0:128], [[-16, 8], [0, 16]], O.is_ge, 0, 1)
    sel("on2", "on2", T.on2[:], T.on2[:], [[16, 9], [0, 16]], O.is_ge, 15, -1)
    sel("on", "BOf", T.BOf[:], T.on[:, 0:128], [[16, 8], [0, 16]], O.is_ge, 15, -1)
    vts("qi", "qa", T.qa[:], T.qi[:], 15, O.bitwise_and)
    vts("qi", "Si", T.Si[:], T.qi[:], 16, O.bitwise_and)
    vms("cxb", T.cxb[:], -float(XB))
    vtc("qa", "qm", T.qm[:], T.qa[:])
    vts("Si", "half1", T.half[:, 1:2], T.Si[:], 0.0625, O.mult)
    vms("c508", T.c508[:], -508.0)
    vts("half1", "half0", T.half[:, 0:1], T.half[:, 1:2], -1.0, O.mult, 1.0, O.add)
    vms("NMe", T.NM[:], 2048.0)
    vms("RS", T.RS[:], BIG)
    vms("ONf", T.ONf[:], 1.0 / 16.0)
    vms("LIM0", T.LIM[:], 18.5)
    vms("NLIM0", T.NLIM[:], -18.5 * STEEP)
    vms("RS", T.RS[:, 0::RUN], -BIG)
    vms("NMe", T.NM[:, RUN - 1::RUN], -30720.0)
    for E in ("Ew", "Ec"):
        for j in (0, RUN - 1):
            vms(E + "z", T[E][:, :, :, j], 0.0, par=True)
    vts("lane qm", "lane", T.lane[:], T.lane[:], T.qm[:], O.add, T.qm[:], O.add)
    for b in range(NB):
        vts("J16 qm NMe", "NM0", T.NM[:, RUN * b + 1:RUN * b + 17], T.J16[:], T.qm[:], O.is_ge, -4096.0, O.mult, par=True)
    vtc("lane RS", "RS", T.RS[:, RUN - 1::RUN], T.lane[:])
    vts("NM0 NMe", "NM", T.NM[:], T.NM[:], -2048.0, O.add)
    for k, s in IDS.items():
        act("IDf", k, T[k][:], T.IDf[:], AF.Copy, scale=s)
    vts("vraw", "vh", T.vh[0:8, :], T.vraw[0:8, :], -float(CMID), O.add)
    for p in range(16):
        mm("PDC vh", "@U:s", T.PU[:, 256:256 + NB], T.PDC[0:8, 15 - p:143 - p], T.vh[0:8, p::16], p == 0, p == 15)
    vtc("traw", "TRu", T.TRu[:], T.traw[:])
    vts("traw", "TR", T.TR[:], T.traw[:], -float(CMID), O.add)
    vts("@U:s", "VH", T.VH[:], T.PU[:, 256:256 + NB], CMID - 0.5, O.add, 0.5, O.mult)
    act("IO0", "IO1", T.IOTA[:, 768:1536], T.IOTA[:, 0:768], AF.Copy, bias=768.0)
    vts("IDf half0", "SWP", T.SWP[:, 0:128], T.IDf[:], T.half[:, 0:1], O.mult)
    vts("IDf half1", "SWP", T.SWP[:, 384:512], T.IDf[:], T.half[:, 1:2], O.mult, par=True)
    vts("sh1 half1", "SWP", T.SWP[:, 128:256], T.sh1[:], T.half[:, 1:2], O.mult, par=True)
    vts("sh0 half0", "SWP", T.SWP[:, 256:384], T.sh0[:], T.half[:, 0:1], O.mult, par=True)
    act("SWP", "SW4", T.SW4[:], T.SWP[:], AF.Copy, scale=4096.0)
    vts("IO0", "IO2", T.IOTA[:, 1536:2304], T.IOTA[:, 0:768], 1536.0, O.add)
    vts("IO0", "IO3", T.IOTA[:, 2304:W], T.IOTA[:, 0:768], 2304.0, O.add)
    IO = "IO0 IO1 IO2 IO3"
    for k, s in (("PDN", -4096.0), ("PD1", 1.0), ("PDS", 1.0 / 16.0)):
        vts("on2", k, T[k][:], T.on2[:], s, O.mult)
    act("BOf", "BO", T.BO[:], T.BOf[:], AF.Sigmoid, scale=STEEP, bias=-STEEP / 2)
    for t in range(T_STEPS):
        sel("ID", "HM%d" % t, T.HM[:, t, :], T.ID[:], [[0, 8], [1, 16]], O.not_equal, -t, 0)
        sel("NID", "NHM%d" % t, T.NHM[:, t, :], T.NID[:], [[0, 8], [1, 16]], O.not_equal, -t, 0)

    Xw, CNw, Z = T.X[:, 0:W], T.CN[:, 0:U], T.Z[:, 0:B]
    DIFF = [("@A", T.PA), ("@B", T.PB), ("@A", T.PA)]
    XG = "xw"
    outs = []

    def unturn(R, bank, P, c0, n, part, S="SWP"):
        for q in range(2):
            mms(bank, P[:, c0 + q:c0 + n:2], [(R + " " + S, T[S][:, 256 * h + 128 * q:256 * h + 128 * q + 128], part(h)) for h in range(2)])

    def turn(R, Wr, o, i, **k):
        op("v", "tr", R, Wr, o, i, **k)

    FW = NB * RUN
    FE = slice(RUN - 1, FW, RUN)

    def calls(t):
        r, last = ROWS[t], t == T_STEPS - 1
        ks = [k for k in range(16) if k != r]
        xw = T.xw[:]
        lim, hm, nhm = "LIM%d" % t, T.HM[:, t, :], T.NHM[:, t, :]
        c = {}
        c["wt"] = lambda: turn("TR", "Wt", T.Wt[:], T.TR[:])
        c["wl"] = lambda: unturn("Wt", "@U:w", T.PU, 384, NB, lambda h: T.Wt[:, 16 * h + r::32])
        c["lu"] = lambda: vts("@U:w", "LU", T.LU[:], T.PU[:, 384:384 + NB], CMID - 0.5, O.add, 0.5, O.mult)
        c["lw"] = lambda: vts("@U:w", "LW", T.LW[:], T.PU[:, 384:384 + NB], float(CMID), O.add)
        c["xw"] = lambda: act(XW + " LW", "xw", xw, Xw.indirect(T.LW[:]))
        c["wf"] = lambda: act("@U:w", "wf", T.wf[:], T.PU[:, 384:384 + NB])
        c["ulf"] = lambda: vts("LU", "ul", T.ul[:], T.LU[:], -float(CMID), O.add)
        c["urow"] = lambda: act(IO + " LU", "urow", T.urow[:], T.IOTA[:].indirect(T.LU[:]))
        c["co"] = lambda: act(CW + " LU", "Co", T.Co[:], CNw.indirect(T.LU[:]), AF.Copy, bias=-float(CMID))
        c["pd"] = lambda: mms("@U:d", T.PU[:, 0:B], [("NID TR", T.NID[:], T.TR[:]), ("ID Co", T.ID[:], T.Co[:])])
        c["mid"] = lambda: act("TR", "Mid", T.Mid[:], T.TR[:], AF.Copy, bias=float(CMID))
        for j in range(4):
            c["cn%d" % j] = lambda j=j: vtc("craw%d" % j, "CN%d" % j, T.CN[:, 384 * j:384 * j + 384], T.craw[:, 384 * j:384 * j + 384])

        c["kr"] = lambda: act(CW + " VH", "Kh", T.Kh[:], CNw.indirect(T.VH[:]), AF.Copy, bias=-float(CMID))
        c["kt"] = lambda: [turn("Kh", "V", T.V[:, :, i], T.Kh[:, 32 * i:32 * i + 32], par=True) for i in range(6)]
        c["kl"] = lambda: unturn("V", "@F:k", T.PF, 256, B, lambda h: T.V[:, 16 * h:16 * h + 16, :])
        c["ko"] = lambda: vts("@F:k", "KT", T.KT[:], T.PF[:, 256:256 + B], float(CMID), O.add)
        c["za"] = lambda: vts("ZI%d" % t, "Za", Z, T["ZI%d" % t][:], -float(XB), O.add)
        c["zb"] = lambda: vts("ZI%d" % t, "Zb", T.Z[:, B:2 * B], T["ZI%d" % t][:], -float(XB), O.add)

        def score(j):
            if not j:
                mm("ID Kh", "@K", T.PK[:, 0:B], T.ID[:], T.Kh[:], True, False)
            for k in (2 * j, 2 * j + 1):
                mm("PDN M%d" % j, "@K", T.PK[:, 0:B], T.PDN[:, 15 - k:143 - k], T.M[:, j, B * (k % 2):B * (k % 2) + B], False, k == 15)

        for j in range(8):
            c["mx%d" % j] = lambda j=j: vtt(XW + " KT Za Zb", "M%d" % j, T.M[:, j, :], Xw.indirect(T.KT[:, 24 * j:24 * j + 24]), T.Z[:], O.max)
            c["s%d" % j] = lambda j=j: score(j)
        c["tp"] = lambda: turn("@K", "key", T.key[:], T.PK[:, 0:B])
        c["sc"] = lambda: scan("RST key", "Sc", T.Sc[:], T.RST[:], T.key[:], O.max, O.min)
        c["ci"] = lambda: vts("Sc", "ci", T.ci[:], T.Sc[:, 15::16], GRID, O.add, GRID, O.subtract)
        c["cm"] = lambda: vtt("Sc ci", "cm", T.cm[:], T.Sc[:, 15::16], T.ci[:], O.subtract)
        c["cw"] = lambda: unturn("cm", "@U:c", T.PU, 448, NB, lambda h: T.cm[:, h::2])
        c["cl"] = lambda: vts("@U:c", "CL", T.CL[:], T.PU[:, 448:448 + NB], float(CMID), O.add)
        c["cf"] = lambda: vtc("@U:c", "cf", T.cf[:], T.PU[:, 448:448 + NB])
        c["crow"] = lambda: act(IO + " CL", "crow", T.crow[:], T.IOTA[:].indirect(T.CL[:]))
        c["xc"] = lambda: act(XW + " CL", "xc", T.xc[:], Xw.indirect(T.CL[:]))
        c["xcut"] = lambda: act("xc", "xcut", T.xcut[:], T.xc[:], AF.Copy, scale=0.5, bias=XB - 0.25)

        def diff(i, h):
            bank, P = DIFF[i]
            for s in range(8 * h, min(8 * h + 8, 15)):
                mms(bank + str(h), P[:, 64 * s:64 * s + 64],
                    [("NID Xg%d" % i, T.NID[:], T.Xg[:, 1024 * i + ks[s]:1024 * i + 1024:16]), ("ID Za", T.ID[:], T.Z[:, 64 * i:64 * i + 64])])

        def thr(i):
            if i in ON_SCALAR:
                act("A%d N%s" % (i, lim), "IND%d" % i, T.IND[:, i, :], T.A2[:, i, :], AF.Sigmoid, scale=STEEP, bias=T.NLIM[:, t:t + 1])
            else:
                vts("A%d %s" % (i, lim), "IND%d" % i, T.IND[:, i, :], T.A2[:, i, :], T.LIM[:, t:t + 1], O.is_gt)

        def count(i):
            mms("@C:n%d" % i, T.PC[:, 64 * i:64 * i + 64],
                [("PD1 IR", T.PD1[:, 15 - r:143 - r], T.IR[:, 64 * i:64 * i + 64])] +
                [("PD1 IND%d" % i, T.PD1[:, 15 - k:143 - k], T.IND[:, i, 64 * s:64 * s + 64]) for s, k in enumerate(ks)])

        for i in range(3):
            bank, P = DIFF[i]
            c["g%d" % i] = lambda i=i: act(XW + " TRu", "Xg%d" % i, T.Xg[:, 1024 * i:1024 * i + 1024], Xw.indirect(T.TRu[:, 64 * i:64 * i + 64]))
            c["d%da" % i] = lambda i=i: diff(i, 0)
            c["d%db" % i] = lambda i=i: diff(i, 1)
            c["ab%d" % i] = lambda i=i, bank=bank, P=P: act("%s0 %s1" % (bank, bank), "A%d" % i, T.A2[:, i, :], P[:, 0:960], AF.Abs)
            c["th%d" % i] = lambda i=i: thr(i)
            c["n%d" % i] = lambda i=i: count(i)
        c["dr"] = lambda: mms("@C:r", T.PC[:, B:2 * B], [("ID Za", T.ID[:], Z), ("NID " + XG, T.NID[:], xw)])
        c["ar"] = lambda: act("@C:r", "AR", T.AR[:], T.PC[:, B:2 * B], AF.Abs)
        c["ir"] = lambda: vts("AR " + lim, "IR", T.IR[:], T.AR[:], T.LIM[:, t:t + 1], O.is_gt)
        c["br"] = lambda: mm("BO IR", "@C:r", T.PC[:, B:2 * B], T.BO[:], T.IR[:], True, True)
        nine = dict(scale=STEEP, bias=-8.5 * STEEP)
        if last:
            c["sr"] = lambda: act("@C:r", "sr", T.sr[:], T.PC[:, B:2 * B], AF.Sigmoid, **nine)
        else:
            c["sr"] = lambda: act("@C:r", "sr Sa", T.sr[:], T.PC[:, B:2 * B], AF.Sigmoid, accum_out=T.Sa[:], **nine)
        c["sev"] = lambda: act("@C:n0 @C:n1 @C:n2", "sev", T.sev[:], T.PC[:, 0:B], AF.Sigmoid, **nine)

        def fold(E, own):
            mm("ID NM", "@F", T.PF[:, 0:FW], T.ID[:], T.NM[:], True, False)
            mm("ID " + own, "@F", T.PF[:, 0:FW:RUN], T.ID[:], T[own][:], False, False)
            for s in reversed(range(NB)):
                nm = "I8" if s else "I4"
                names = " ".join("%s%d" % (E, b) for b in range(s, NB))
                mm(names + " %sz %s" % (E, nm), "@F", T.PF[:, RUN * s:FW], T[nm][:], T[E][:, s:NB, NB - 1 - s, :], False, s == 0)

        for n, E, F, row, col, own in (("w", "Ew", "Fw", "urow", "ul", "wf"), ("c", "Ec", "Fc", "crow", "cf", "cf")):
            for b in range(NB):
                c["e%s%d" % (n, b)] = lambda b=b, E=E, row=row, col=col: vts(
                    row + " " + col, "%s%d" % (E, b), T[E][:, b, NB - 1 - b:NB, 1:17], T[row][:, 0:16 * b + 16], T[col][:, b:b + 1], O.is_equal)
            c["fo" + n] = lambda E=E, own=own: fold(E, own)
            c["f" + n] = lambda F=F: scan("RS @F", F, T[F][:], T.RS[:], T.PF[:, 0:FW], O.min, O.max)
        c["lh"] = lambda: vts("Fw", "LH", T.LH[:], T.Fw[:, FE], float(CMID), O.add)
        c["st"] = lambda: turn("sr", "St", T.St[:], T.sr[:])
        c["sk"] = lambda: unturn("St", "@U:s", T.PU, 256, NB, lambda h: T.St[:, 16 * h::32], "SW4")
        c["lcf"] = lambda: vtt("@U:s Fw", "LCf", T.LCf[:], T.PU[:, 256:256 + NB], T.Fw[:, FE], O.add)
        c["lc"] = lambda: vts("LCf", "LC", T.LC[:], T.LCf[:], CMID - 0.5, O.add, 0.5, O.mult)
        c["ul"] = lambda: vts("Fc", "UL", T.UL[:], T.Fc[:, FE], float(CMID), O.add)

        c["p1"] = lambda: mms("@C:r", T.PC[:, B:2 * B], [("NHI " + XG, T.NHI[:], xw), ("NHI Za", T.NHI[:], Z), ("I512 sr", T.I512[:], T.sr[:])])
        c["p2"] = lambda: mms("@F:k", T.PF[:, 256:256 + B], [("ID " + XG, T.ID[:], xw), ("ID c508", T.ID[:], T.c508[:]), ("I512 sr", T.I512[:], T.sr[:])])
        c["t1"] = lambda: act("@C:r", "t1", T.t1[:], T.PC[:, B:2 * B], AF.Relu, scale=-1.0, bias=XB - 0.25)
        c["t2"] = lambda: vts("@F:k", "t2", T.t2[:], T.PF[:, 256:256 + B], 63.0, O.min, -float(XB), O.max)
        c["xr"] = lambda: vtt("t1 t2 LH", XW, T.X[:].indirect(T.LH[:]), T.t1[:], T.t2[:], O.add)
        c["xk"] = lambda: vtt("xcut cxb UL", XW, T.X[:].indirect(T.UL[:]), T.xcut[:], T.cxb[:], O.add)

        c["q1"] = lambda: mms("@B0", T.PB[:, 0:B], [("HM%d Kh" % t, hm, T.Kh[:]), ("NHM%d TR" % t, nhm, T.TR[:])])
        c["q2"] = lambda: mms("@B1", T.PB[:, 512:512 + B], [("HM%d TR" % t, hm, T.TR[:]), ("PDS crow", T.PDS[:, 15 - t:143 - t], T.crow[:])] +
                              ([("ID cmid", T.ID[:], T.cmid[:])] if last else []))
        c["cd"] = lambda: vtt("@U:d sev", "cD", T.cD[:], T.PU[:, 0:B], T.sev[:], O.mult)
        c["td"] = lambda: vtt("@B0 sev", "tD", T.tD[:], T.PB[:, 0:B], T.sev[:], O.mult)
        c["cs"] = lambda: vtt("cD Mid LC", CW, T.CN[:].indirect(T.LC[:]), T.cD[:], T.Mid[:], O.add)

        def store(R, name, o, i, n):
            w = o.shape[1] // n
            for j in range(n):
                outs.append(dma("s", R, "%s%d" % (name, j), o[:, w * j:w * j + w], i[:, w * j:w * j + w]))

        if last:
            c["tr"] = lambda: vtt("@B1 tD", "TF", T.TF[:], T.PB[:, 512:512 + B], T.tD[:], O.add)
            c["ox"] = lambda: store(XW, "yx", T.yx, T.X, 2)
            c["ol"] = lambda: store(CW, "yl", T.yl, T.CN, 2)
            c["og"] = lambda: store("TF", "yg", T.yg, T.TF, 1)
            return c
        c["tr"] = lambda: vtt("@B1 tD", "TR", T.TR[:], T.PB[:, 512:512 + B], T.tD[:], O.add)
        c["tru"] = lambda: vts("TR", "TRu", T.TRu[:], T.TR[:], float(CMID), O.add)
        c["vh"] = lambda: vts("@U:c", "VH", T.VH[:], T.PU[:, 448:448 + NB], CMID - 0.5, O.add, 0.5, O.mult)
        c["sa"] = lambda: mm("ONf Sa", "@U:a", T.PU[:, 320:321], T.ONf[:], T.Sa[:], True, True)
        c["si"] = lambda: vtc("@U:a", "Si", T.Si[:], T.PU[:, 320:321])
        c["sj"] = lambda: vts("Si", "Sj", T.Sj[:], T.Si[:], 3, O.bitwise_and)
        c["lim"] = lambda: vts("Sj", "LIM%d" % (t + 1), T.LIM[:, t + 1:t + 2], T.Sj[:], 18.5, O.add)
        c["nlim"] = lambda: vts("Sj", "NLIM%d" % (t + 1), T.NLIM[:, t + 1:t + 2], T.Sj[:], 18.5, O.add, -STEEP, O.mult)
        zo, zi = "ZO%d" % (t + 1), "ZI%d" % (t + 1)
        c["gs"] = lambda: mms("@K", T.PK[:, B:2 * B], [("ID Za", T.ID[:], Z), ("ID xc", T.ID[:], T.xc[:])])
        c["zn"] = lambda: act("@K", zo, T[zo][:], T.PK[:, B:2 * B], AF.Copy, scale=0.5, bias=XB - 0.25)

        def send():
            dst = T.cores[(rank + 1 + t % (N - 1)) % N]
            rid, pid, _e = topo.addr(dst)
            need("g", wr[zo][0], wr[zo][1])
            g.remote_dma(T[zi][:], T[zo][:], T.sem["zs%d" % (t + 1)], T.sem.zsent, pid, rid, topo.mask(core, dst))
            src = T.cores[(rank - 1 - t % (N - 1)) % N]
            note("zs%d" % (t + 1), len(topo.engines(src, core)), [], [zi])

        c["send"] = send
        return c

    C = [calls(t) for t in range(T_STEPS)] + [{}]
    for name in FIRST.split():
        C[0][name]()
    for t in range(T_STEPS):
        for name in STEP.split():
            c = C[t + 1] if name[0] == "+" else C[t]
            if name.strip("+") in c:
                c[name.strip("+")]()
    for s in outs:
        need("s", s, 16)
    g.wait_ge(T.sem.zsent, sum(len(topo.engines(core, T.cores[(rank + 1 + t % (N - 1)) % N])) for t in range(T_STEPS - 1)))
